import numpy as np
import ml_dtypes


def mxq(x, axis, fmt="e4m3"):
    dtype, down = {"e4m3": (ml_dtypes.float8_e4m3fn, 7), "e5m2": (ml_dtypes.float8_e5m2, 14)}[fmt]
    v = np.moveaxis(np.asarray(x, np.float32).astype(ml_dtypes.bfloat16).astype(np.float64), axis, -1)
    blocks = v.reshape(v.shape[:-1] + (-1, 32))
    amax = np.abs(blocks).max(-1, keepdims=True)
    byte = np.maximum(np.where(amax > 0, np.frexp(amax)[1] - 1 + 127, 0) - down, 1)
    scale = np.exp2(byte - 127.0)
    codes = (blocks / scale).astype(np.float32).astype(dtype).astype(np.float64)
    return np.moveaxis((codes * scale).reshape(v.shape), -1, axis)


WIDE = False


def mx_kscale(k):
    if not WIDE:
        return np.ones(k)
    levels = np.array([24, -24, 12, -12, 0])
    if k % 512:
        return np.exp2(np.random.permutation(np.resize(levels, k // 32))).repeat(32)
    a = np.empty((k // 512, 16))
    for p in range(k // 512):
        a[p, :8] = np.random.permutation(np.resize(levels, 8))
        for g in range(8):
            far = levels[np.abs(levels - a[p, g]) >= 10]
            a[p, g + 8] = far[np.random.randint(len(far))]
    return np.exp2(a.ravel()).repeat(32)


def f64(x):
    return np.asarray(x).astype(np.float64)


def striped(idx):
    return np.tile(idx.reshape(-1, 16).T, (8, 1)).astype(np.uint16)


def unstriped(offs):
    return offs[:16].T.reshape(-1).astype(np.int64)


E2M1 = np.array([0.0, 0.5, 1.0, 1.5, 2.0, 3.0, 4.0, 6.0, -0.0, -0.5, -1.0, -1.5, -2.0, -3.0, -4.0, -6.0])


def pack_weight(w, fmt):
    k, n = w.shape
    w = f64(np.asarray(w, np.float32).astype(ml_dtypes.bfloat16)).reshape(k // 32, 32, n)
    amax = np.abs(w).max(1)
    if fmt == "e4m3":
        byte = np.frexp(amax)[1] - 1 + 127 - 7
    else:
        mant, ex = np.frexp(amax / 6.0)
        byte = np.where(mant > 0.5, ex, ex - 1) + 127
    byte = np.clip(np.where(amax > 0, byte, 1), 1, 254)
    scaled = (w * np.exp2(127.0 - byte)[:, None, :]).reshape(k, n).astype(np.float32)
    by_word = np.ascontiguousarray(scaled.reshape(k // 512, 128, 4, n).transpose(0, 1, 3, 2))
    if fmt == "e4m3":
        words = by_word.astype(ml_dtypes.float8_e4m3fn).view(np.uint8)
    else:
        c = by_word.astype(ml_dtypes.float4_e2m1fn).view(np.uint8) & 0xF
        words = (c[..., 0::2] | (c[..., 1::2] << 4)).reshape(k // 512, 128, 2 * n)
    return np.ascontiguousarray(words), np.ascontiguousarray(byte.astype(np.uint8).reshape(k // 512, 16, n))


def unpack_weight(words, scales, fmt):
    g, _, n = scales.shape
    words = np.ascontiguousarray(words).reshape(g, 128, n, -1)
    if fmt == "e4m3":
        vals = words.view(ml_dtypes.float8_e4m3fn).astype(np.float64)
    else:
        nib = np.empty((g, 128, n, 4), np.uint8)
        nib[..., 0::2] = words & 0xF
        nib[..., 1::2] = words >> 4
        vals = E2M1[nib]
    vals = vals * np.repeat(np.exp2(scales.astype(np.float64) - 127.0), 8, axis=1)[..., None]
    return vals.transpose(0, 1, 3, 2).reshape(g * 512, n)


K, R, M, T, N, J = 512, 512, 512, 2048, 512, 1024


def setup_inputs():
    n = np.random.standard_normal
    u = mx_kscale(R)[:, None]
    s = mx_kscale(K)[:, None]
    p_w8 = pack_weight(n((K, R)) / np.sqrt(K) / s / u.T, "e4m3")
    p_tab = pack_weight(n((R, T)) * u, "e4m3")
    p_wv4 = pack_weight(n((R, N)) / np.sqrt(R) / u, "e2m1")
    return {
        "x": (n((K, M)) * s).astype(np.float32),
        "w8_words": p_w8[0],
        "w8_scales": p_w8[1],
        "tab_words": p_tab[0],
        "tab_scales": p_tab[1],
        "wv4_words": p_wv4[0],
        "wv4_scales": p_wv4[1],
        "wvd": (0.4 * (n((R, N)) / np.sqrt(R) / u)).astype(np.float32),
        "offs": striped(np.random.permutation(T)[:J]),
    }


def reference(x, w8_words, w8_scales, tab_words, tab_scales, wv4_words, wv4_scales, wvd, offs):
    idx = unstriped(offs)
    x_ = mxq(f64(x), 0, "e4m3")
    w8_ = unpack_weight(w8_words, w8_scales, "e4m3")
    qa = w8_.T @ x_
    qa_ = mxq(qa, 0, "e4m3")
    tab_ = unpack_weight(tab_words, tab_scales, "e4m3")[:, idx]
    sc = qa_.T @ tab_
    wv4_ = unpack_weight(wv4_words, wv4_scales, "e2m1")
    wvd_ = mxq(f64(wvd), 0, "e4m3")
    vv = wv4_.T @ tab_ + wvd_.T @ tab_
    return sc * 0.03125, vv

@@ -1,0 +1,181 @@
+from contextlib import ExitStack
+
+import concourse.mybir as mybir
+
+K, R, M, T, N, J = 512, 512, 512, 2048, 512, 1024
+FLOPS = 2 * K * R * M + 2 * R * M * J + 2 * 2 * R * N * J
+
+F32 = mybir.dt.float32
+BF16 = mybir.dt.bfloat16
+I32 = mybir.dt.int32
+U32 = mybir.dt.uint32
+U16 = mybir.dt.uint16
+U8 = mybir.dt.uint8
+FP8X4 = mybir.dt.float8_e4m3fn_x4
+FP4X4 = mybir.dt.float4_e2m1fn_x4
+COPY = mybir.ActivationFunctionType.Copy
+MULT = mybir.AluOpType.mult
+
+P = 128
+PACK = 4
+BANK = 512
+HALF = 256
+SCORE_SCALE = 0.03125
+
+
+def tile_list_mlat_dl_scale_kernel(tc, x, w8_words, w8_scales, tab_words, tab_scales, wv4_words, wv4_scales, wvd, offs, out_0, out_1):
+    nc = tc.nc
+    with ExitStack() as ctx:
+        keep = ctx.enter_context(tc.tile_pool(name="keep", bufs=1))
+        outs = ctx.enter_context(tc.tile_pool(name="outs", bufs=8))
+        psum_q = ctx.enter_context(tc.psum_pool(name="psum_q", bufs=2))
+        psum_o = ctx.enter_context(tc.psum_pool(name="psum_o", bufs=6))
+
+        def tile(name, shape, dtype):
+            return keep.tile(shape, dtype, name=name, align_bytes=64)
+
+        def load_scale_rows(queue, plane, rows):
+            for q in range(4):
+                queue.dma_start(out=plane[32 * q : 32 * q + 4, :].bitcast(I32), in_=rows[0, 4 * q : 4 * q + 4, :].bitcast(I32))
+
+        def load_rows(name, src, half):
+            raw = tile(name, [P, PACK, HALF], F32)
+            nc.sync.dma_start(out=raw[:], in_=src.rearrange("(p i) c -> p i c", i=PACK)[:, :, half * HALF : (half + 1) * HALF])
+            return raw
+
+        tab_plane = tile("tab_plane", [P, T], U8)
+        w8_plane = tile("w8_plane", [P, R], U8)
+        wv4_plane = tile("wv4_plane", [P, N], U8)
+        for plane in (tab_plane, w8_plane, wv4_plane):
+            nc.vector.memset(plane[:].bitcast(I32), 0)
+
+        w8_raw = tile("w8_raw", [P, R], I32)
+        nc.sync.dma_start(out=w8_raw[:], in_=w8_words[0].rearrange("p r i -> p (r i)").bitcast(I32))
+        offsets = keep.tile([P, J // 16], U16, name="offsets")
+        nc.sync.dma_start(offsets[:], offs)
+        wv4_codes = tile("wv4_codes", [P, 2 * N], U8)
+        nc.sync.dma_start(out=wv4_codes[:].bitcast(I32), in_=wv4_words[0].bitcast(I32))
+        load_scale_rows(nc.sync, tab_plane, tab_scales)
+        x_raw0 = load_rows("x_raw0", x, 0)
+        load_scale_rows(nc.sync, w8_plane, w8_scales)
+        tab_codes = tile("tab_codes", [P, T], U32)
+        nc.sync.dma_start(out=tab_codes[:].bitcast(I32), in_=tab_words[0].rearrange("p t i -> p (t i)").bitcast(I32))
+        wvd_raw = [load_rows("wvd_raw%d" % h, wvd, h) for h in range(2)]
+        x_raw1 = load_rows("x_raw1", x, 1)
+        load_scale_rows(nc.gpsimd, wv4_plane, wv4_scales)
+
+        def interleave(name, engine, raw, c0, width):
+            grouped = tile(name, [P, width, PACK], BF16)
+            dst = grouped[:].rearrange("p (c e) i -> p c i e", e=4)
+            src = raw[:, :, c0 : c0 + width].rearrange("p i (c e) -> p c i e", e=4)
+            if engine == "scalar":
+                nc.scalar.copy(out=dst, in_=src)
+            else:
+                nc.vector.tensor_copy(out=dst, in_=src)
+            return grouped
+
+        def quantize(name, grouped):
+            width = grouped.shape[1]
+            codes = tile(name + "_codes", [P, width], U32)
+            plane = tile(name + "_plane", [P, width], U8)
+            nc.vector.quantize_mx(out=codes[:].bitcast(FP8X4), scales=plane[:], in_=grouped[:].rearrange("p c i -> p (c i)"))
+            return codes, plane
+
+        def gather(name, window, dtype, half):
+            picked = tile(name, [P, BANK], dtype)
+            cols = BANK // 16
+            nc.vector.tensor_copy(picked[:], window[:].indirect(offsets[:, half * cols : (half + 1) * cols]))
+            return picked
+
+        w8_codes = tile("w8_codes", [P, R], I32)
+        nc.vector.tensor_copy(
+            out=w8_codes[:].rearrange("p (i c e) -> p c i e", i=PACK, e=4),
+            in_=w8_raw[:].rearrange("p (c e i) -> p c i e", i=PACK, e=4),
+        )
+        v_plane = [gather("v_plane%d" % h, tab_plane, U8, h) for h in range(2)]
+        w8_sorted = tile("w8_sorted", [P, R], U8)
+        nc.vector.tensor_copy(
+            out=w8_sorted[:].rearrange("p (i c e) -> p c i e", i=PACK, e=16),
+            in_=w8_plane[:].rearrange("p (c e i) -> p c i e", i=PACK, e=16),
+        )
+
+        def project(mt, xq, c0, engine):
+            codes, plane = xq
+            bank = psum_q.tile([P, PACK, P], F32, name="qa_bank")
+            for i in range(PACK):
+                cols = slice(i * P, (i + 1) * P)
+                nc.tensor.matmul_mx(
+                    out=bank[:, i, :], lhsT=w8_codes[:, cols].bitcast(FP8X4), lhsT_scale=w8_sorted[:, cols],
+                    rhs=codes[:, c0 : c0 + P].bitcast(FP8X4), rhs_scale=plane[:, c0 : c0 + P], start=True, stop=True,
+                )
+            grouped = tile("qa_grouped%d" % mt, [P, P, PACK], BF16)
+            src = bank[:].rearrange("p i m -> p m i")
+            if engine == "scalar":
+                nc.scalar.copy(out=grouped[:], in_=src)
+            else:
+                nc.vector.tensor_copy(out=grouped[:], in_=src)
+            return grouped
+
+        def store(bank, dst, engine, scale):
+            result = outs.tile([P, BANK], F32, name="result")
+            if engine == "scalar":
+                nc.scalar.activation(out=result[:], in_=bank[:], func=COPY, scale=scale)
+            else:
+                nc.vector.tensor_scalar(out=result[:], in0=bank[:], scalar1=scale, scalar2=None, op0=MULT)
+            nc.sync.dma_start(out=dst, in_=result[:])
+
+        def scores(mt, qa, h, engine):
+            codes, plane = qa
+            bank = psum_o.tile([P, BANK], F32, name="out_bank")
+            nc.tensor.matmul_mx(
+                out=bank[:], lhsT=codes[:].bitcast(FP8X4), lhsT_scale=plane[:],
+                rhs=v_codes[h][:].bitcast(FP8X4), rhs_scale=v_plane[h][:], start=True, stop=True,
+            )
+            store(bank, out_0[mt * P : (mt + 1) * P, h * BANK : (h + 1) * BANK], engine, SCORE_SCALE)
+
+        def values(nt, wq, c0, h, engine):
+            codes, plane = wq
+            bank = psum_o.tile([P, BANK], F32, name="out_bank")
+            nc.tensor.matmul_mx(
+                out=bank[:], lhsT=wv4_codes[:, 2 * nt * P : 2 * (nt + 1) * P].bitcast(FP4X4),
+                lhsT_scale=wv4_plane[:, nt * P : (nt + 1) * P],
+                rhs=v_codes[h][:].bitcast(FP8X4), rhs_scale=v_plane[h][:], start=True, stop=False,
+            )
+            nc.tensor.matmul_mx(
+                out=bank[:], lhsT=codes[:, c0 : c0 + P].bitcast(FP8X4), lhsT_scale=plane[:, c0 : c0 + P],
+                rhs=v_codes[h][:].bitcast(FP8X4), rhs_scale=v_plane[h][:], start=False, stop=True,
+            )
+            store(bank, out_1[nt * P : (nt + 1) * P, h * BANK : (h + 1) * BANK], engine, 1.0)
+
+        xg = [interleave("x_grouped%d" % mt, "scalar", x_raw0, mt * P, P) for mt in range(2)]
+        xq = [quantize("x%d" % mt, xg[mt]) for mt in range(2)]
+        qg = [project(mt, xq[mt], 0, "scalar") for mt in range(2)]
+        v_codes = [gather("v_codes0", tab_codes, U32, 0)]
+        qa = [quantize("qa%d" % mt, qg[mt]) for mt in range(2)]
+        wg0 = interleave("wvd_grouped0", "scalar", wvd_raw[0], 0, P)
+        v_codes.append(gather("v_codes1", tab_codes, U32, 1))
+        for h in range(2):
+            for mt in range(2):
+                scores(mt, qa[mt], h, "scalar")
+        wq0 = quantize("wvd0", wg0)
+        wg1 = interleave("wvd_grouped1", "vector", wvd_raw[0], P, P)
+        wg23 = interleave("wvd_grouped23", "vector", wvd_raw[1], 0, HALF)
+        wq1 = quantize("wvd1", wg1)
+        xg23 = interleave("x_grouped23", "vector", x_raw1, 0, HALF)
+        wq23 = quantize("wvd23", wg23)
+        xq23 = quantize("x23", xg23)
+        for h in range(2):
+            values(0, wq0, 0, h, "scalar")
+        for h in range(2):
+            values(1, wq1, 0, h, "scalar")
+        qg2 = project(2, xq23, 0, "vector")
+        for h in range(2):
+            values(2, wq23, 0, h, "scalar")
+        qg3 = project(3, xq23, P, "vector")
+        qa2 = quantize("qa2", qg2)
+        values(3, wq23, P, 0, "scalar")
+        qa3 = quantize("qa3", qg3)
+        values(3, wq23, P, 1, "vector")
+        for mt, q in ((2, qa2), (3, qa3)):
+            scores(mt, q, 0, "scalar")
+            scores(mt, q, 1, "vector")

@@ -31,8 +31,8 @@ def tile_list_mlat_dl_scale_kernel(tc, x, w8_words, w8_scales, tab_words, tab_sc
         psum_q = ctx.enter_context(tc.psum_pool(name="psum_q", bufs=2))
         psum_o = ctx.enter_context(tc.psum_pool(name="psum_o", bufs=6))
 
-        def tile(name, shape, dtype):
-            return keep.tile(shape, dtype, name=name, align_bytes=64)
+        def tile(name, shape, dtype, tag=None):
+            return keep.tile(shape, dtype, name=name, tag=tag or name, align_bytes=64)
 
         def load_scale_rows(queue, plane, rows):
             for q in range(4):
@@ -46,23 +46,25 @@ def tile_list_mlat_dl_scale_kernel(tc, x, w8_words, w8_scales, tab_words, tab_sc
         tab_plane = tile("tab_plane", [P, T], U8)
         w8_plane = tile("w8_plane", [P, R], U8)
         wv4_plane = tile("wv4_plane", [P, N], U8)
-        for plane in (tab_plane, w8_plane, wv4_plane):
-            nc.vector.memset(plane[:].bitcast(I32), 0)
+        nc.vector.memset(tab_plane[:].bitcast(I32), 0)
+        nc.vector.memset(w8_plane[:].bitcast(I32), 0)
+        nc.gpsimd.memset(wv4_plane[:].bitcast(I32), 0)
+        load_scale_rows(nc.gpsimd, wv4_plane, wv4_scales)
 
-        w8_raw = tile("w8_raw", [P, R], I32)
-        nc.sync.dma_start(out=w8_raw[:], in_=w8_words[0].rearrange("p r i -> p (r i)").bitcast(I32))
+        x_raw0 = load_rows("x_raw0", x, 0)
         offsets = keep.tile([P, J // 16], U16, name="offsets")
         nc.sync.dma_start(offsets[:], offs)
-        wv4_codes = tile("wv4_codes", [P, 2 * N], U8)
-        nc.sync.dma_start(out=wv4_codes[:].bitcast(I32), in_=wv4_words[0].bitcast(I32))
         load_scale_rows(nc.sync, tab_plane, tab_scales)
-        x_raw0 = load_rows("x_raw0", x, 0)
-        load_scale_rows(nc.sync, w8_plane, w8_scales)
+        w8_raw = tile("w8_raw", [P, R], I32)
+        nc.sync.dma_start(out=w8_raw[:], in_=w8_words[0].rearrange("p r i -> p (r i)").bitcast(I32))
         tab_codes = tile("tab_codes", [P, T], U32)
         nc.sync.dma_start(out=tab_codes[:].bitcast(I32), in_=tab_words[0].rearrange("p t i -> p (t i)").bitcast(I32))
-        wvd_raw = [load_rows("wvd_raw%d" % h, wvd, h) for h in range(2)]
+        load_scale_rows(nc.sync, w8_plane, w8_scales)
+        wvd_raw0 = load_rows("wvd_raw0", wvd, 0)
+        wv4_codes = tile("wv4_codes", [P, 2 * N], U8)
+        nc.sync.dma_start(out=wv4_codes[:].bitcast(I32), in_=wv4_words[0].bitcast(I32))
         x_raw1 = load_rows("x_raw1", x, 1)
-        load_scale_rows(nc.gpsimd, wv4_plane, wv4_scales)
+        wvd_raw1 = load_rows("wvd_raw1", wvd, 1)
 
         def interleave(name, engine, raw, c0, width):
             grouped = tile(name, [P, width, PACK], BF16)
@@ -74,30 +76,33 @@ def tile_list_mlat_dl_scale_kernel(tc, x, w8_words, w8_scales, tab_words, tab_sc
                 nc.vector.tensor_copy(out=dst, in_=src)
             return grouped
 
-        def quantize(name, grouped):
+        def quantize(name, grouped, tag=None):
             width = grouped.shape[1]
-            codes = tile(name + "_codes", [P, width], U32)
+            codes = tile(name + "_codes", [P, width], U32, tag)
             plane = tile(name + "_plane", [P, width], U8)
             nc.vector.quantize_mx(out=codes[:].bitcast(FP8X4), scales=plane[:], in_=grouped[:].rearrange("p c i -> p (c i)"))
             return codes, plane
 
-        def gather(name, window, dtype, half):
-            picked = tile(name, [P, BANK], dtype)
+        def gather(name, window, dtype, half, tag=None):
+            picked = tile(name, [P, BANK], dtype, tag)
             cols = BANK // 16
             nc.vector.tensor_copy(picked[:], window[:].indirect(offsets[:, half * cols : (half + 1) * cols]))
             return picked
 
+        xg01 = interleave("x_grouped01", "scalar", x_raw0, 0, HALF)
+        v_plane = [gather("v_plane%d" % h, tab_plane, U8, h) for h in range(2)]
         w8_codes = tile("w8_codes", [P, R], I32)
         nc.vector.tensor_copy(
             out=w8_codes[:].rearrange("p (i c e) -> p c i e", i=PACK, e=4),
             in_=w8_raw[:].rearrange("p (c e i) -> p c i e", i=PACK, e=4),
         )
-        v_plane = [gather("v_plane%d" % h, tab_plane, U8, h) for h in range(2)]
+        xq01 = quantize("x01", xg01, "tab_plane")
         w8_sorted = tile("w8_sorted", [P, R], U8)
         nc.vector.tensor_copy(
             out=w8_sorted[:].rearrange("p (i c e) -> p c i e", i=PACK, e=16),
             in_=w8_plane[:].rearrange("p (c e i) -> p c i e", i=PACK, e=16),
         )
+        v_codes = [gather("v_codes0", tab_codes, U32, 0, "w8_plane")]
 
         def project(mt, xq, c0, engine):
             codes, plane = xq
@@ -137,45 +142,35 @@ def tile_list_mlat_dl_scale_kernel(tc, x, w8_words, w8_scales, tab_words, tab_sc
             codes, plane = wq
             bank = psum_o.tile([P, BANK], F32, name="out_bank")
             nc.tensor.matmul_mx(
-                out=bank[:], lhsT=wv4_codes[:, 2 * nt * P : 2 * (nt + 1) * P].bitcast(FP4X4),
-                lhsT_scale=wv4_plane[:, nt * P : (nt + 1) * P],
+                out=bank[:], lhsT=codes[:, c0 : c0 + P].bitcast(FP8X4), lhsT_scale=plane[:, c0 : c0 + P],
                 rhs=v_codes[h][:].bitcast(FP8X4), rhs_scale=v_plane[h][:], start=True, stop=False,
             )
             nc.tensor.matmul_mx(
-                out=bank[:], lhsT=codes[:, c0 : c0 + P].bitcast(FP8X4), lhsT_scale=plane[:, c0 : c0 + P],
+                out=bank[:], lhsT=wv4_codes[:, 2 * nt * P : 2 * (nt + 1) * P].bitcast(FP4X4),
+                lhsT_scale=wv4_plane[:, nt * P : (nt + 1) * P],
                 rhs=v_codes[h][:].bitcast(FP8X4), rhs_scale=v_plane[h][:], start=False, stop=True,
             )
             store(bank, out_1[nt * P : (nt + 1) * P, h * BANK : (h + 1) * BANK], engine, 1.0)
 
-        xg = [interleave("x_grouped%d" % mt, "scalar", x_raw0, mt * P, P) for mt in range(2)]
-        xq = [quantize("x%d" % mt, xg[mt]) for mt in range(2)]
-        qg = [project(mt, xq[mt], 0, "scalar") for mt in range(2)]
-        v_codes = [gather("v_codes0", tab_codes, U32, 0)]
-        qa = [quantize("qa%d" % mt, qg[mt]) for mt in range(2)]
-        wg0 = interleave("wvd_grouped0", "scalar", wvd_raw[0], 0, P)
-        v_codes.append(gather("v_codes1", tab_codes, U32, 1))
+        qg = [project(mt, xq01, mt * P, "scalar") for mt in range(2)]
+        wg01 = interleave("wvd_grouped01", "vector", wvd_raw0, 0, HALF)
+        qa = [quantize("qa0", qg[0])]
+        wq01 = quantize("wvd01", wg01)
+        qa.append(quantize("qa1", qg[1]))
+        v_codes.append(gather("v_codes1", tab_codes, U32, 1, "qa_grouped1"))
         for h in range(2):
-            for mt in range(2):
-                scores(mt, qa[mt], h, "scalar")
-        wq0 = quantize("wvd0", wg0)
-        wg1 = interleave("wvd_grouped1", "vector", wvd_raw[0], P, P)
-        wg23 = interleave("wvd_grouped23", "vector", wvd_raw[1], 0, HALF)
-        wq1 = quantize("wvd1", wg1)
+            for t in range(2):
+                scores(t, qa[t], h, "scalar")
+                values(t, wq01, t * P, h, "scalar")
         xg23 = interleave("x_grouped23", "vector", x_raw1, 0, HALF)
-        wq23 = quantize("wvd23", wg23)
+        wg23 = interleave("wvd_grouped23", "vector", wvd_raw1, 0, HALF)
         xq23 = quantize("x23", xg23)
-        for h in range(2):
-            values(0, wq0, 0, h, "scalar")
-        for h in range(2):
-            values(1, wq1, 0, h, "scalar")
-        qg2 = project(2, xq23, 0, "vector")
-        for h in range(2):
-            values(2, wq23, 0, h, "scalar")
-        qg3 = project(3, xq23, P, "vector")
-        qa2 = quantize("qa2", qg2)
-        values(3, wq23, P, 0, "scalar")
-        qa3 = quantize("qa3", qg3)
-        values(3, wq23, P, 1, "vector")
-        for mt, q in ((2, qa2), (3, qa3)):
-            scores(mt, q, 0, "scalar")
-            scores(mt, q, 1, "vector")
+        wq23 = quantize("wvd23", wg23)
+        qg = qg + [project(mt, xq23, (mt - 2) * P, "vector") for mt in (2, 3)]
+        qa = qa + [quantize("qa%d" % mt, qg[mt]) for mt in (2, 3)]
+        for t in (2, 3):
+            values(t, wq23, (t - 2) * P, 0, "scalar")
+            values(t, wq23, (t - 2) * P, 1, "vector")
+        for t in (2, 3):
+            scores(t, qa[t], 0, "vector")
+            scores(t, qa[t], 1, "scalar")

@@ -14,7 +14,6 @@ U8 = mybir.dt.uint8
 FP8X4 = mybir.dt.float8_e4m3fn_x4
 FP4X4 = mybir.dt.float4_e2m1fn_x4
 COPY = mybir.ActivationFunctionType.Copy
-MULT = mybir.AluOpType.mult
 
 P = 128
 PACK = 4
@@ -27,47 +26,43 @@ def tile_list_mlat_dl_scale_kernel(tc, x, w8_words, w8_scales, tab_words, tab_sc
     nc = tc.nc
     with ExitStack() as ctx:
         keep = ctx.enter_context(tc.tile_pool(name="keep", bufs=1))
-        outs = ctx.enter_context(tc.tile_pool(name="outs", bufs=8))
-        psum_q = ctx.enter_context(tc.psum_pool(name="psum_q", bufs=2))
-        psum_o = ctx.enter_context(tc.psum_pool(name="psum_o", bufs=6))
+        psum_q = ctx.enter_context(tc.psum_pool(name="psum_q", bufs=3))
+        psum_o = ctx.enter_context(tc.psum_pool(name="psum_o", bufs=5))
 
         def tile(name, shape, dtype, tag=None):
             return keep.tile(shape, dtype, name=name, tag=tag or name, align_bytes=64)
 
-        def load_scale_rows(queue, plane, rows):
+        def load_scale_rows(plane, rows):
             for q in range(4):
-                queue.dma_start(out=plane[32 * q : 32 * q + 4, :].bitcast(I32), in_=rows[0, 4 * q : 4 * q + 4, :].bitcast(I32))
+                nc.sync.dma_start(out=plane[32 * q : 32 * q + 4, :].bitcast(I32), in_=rows[0, 4 * q : 4 * q + 4, :].bitcast(I32))
 
-        def load_rows(name, src, half):
-            raw = tile(name, [P, PACK, HALF], F32)
-            nc.sync.dma_start(out=raw[:], in_=src.rearrange("(p i) c -> p i c", i=PACK)[:, :, half * HALF : (half + 1) * HALF])
+        def load_rows(name, src):
+            raw = tile(name, [P, PACK, src.shape[1]], F32)
+            nc.sync.dma_start(out=raw[:], in_=src.rearrange("(p i) c -> p i c", i=PACK))
             return raw
 
         tab_plane = tile("tab_plane", [P, T], U8)
         w8_plane = tile("w8_plane", [P, R], U8)
         wv4_plane = tile("wv4_plane", [P, N], U8)
-        nc.vector.memset(tab_plane[:].bitcast(I32), 0)
-        nc.vector.memset(w8_plane[:].bitcast(I32), 0)
-        nc.gpsimd.memset(wv4_plane[:].bitcast(I32), 0)
-        load_scale_rows(nc.gpsimd, wv4_plane, wv4_scales)
+        for plane in (tab_plane, w8_plane, wv4_plane):
+            nc.vector.memset(plane[:].bitcast(I32), 0)
 
-        x_raw0 = load_rows("x_raw0", x, 0)
         offsets = keep.tile([P, J // 16], U16, name="offsets")
         nc.sync.dma_start(offsets[:], offs)
-        load_scale_rows(nc.sync, tab_plane, tab_scales)
         w8_raw = tile("w8_raw", [P, R], I32)
         nc.sync.dma_start(out=w8_raw[:], in_=w8_words[0].rearrange("p r i -> p (r i)").bitcast(I32))
+        load_scale_rows(tab_plane, tab_scales)
+        x_raw = load_rows("x_raw", x)
+        load_scale_rows(w8_plane, w8_scales)
         tab_codes = tile("tab_codes", [P, T], U32)
         nc.sync.dma_start(out=tab_codes[:].bitcast(I32), in_=tab_words[0].rearrange("p t i -> p (t i)").bitcast(I32))
-        load_scale_rows(nc.sync, w8_plane, w8_scales)
-        wvd_raw0 = load_rows("wvd_raw0", wvd, 0)
         wv4_codes = tile("wv4_codes", [P, 2 * N], U8)
         nc.sync.dma_start(out=wv4_codes[:].bitcast(I32), in_=wv4_words[0].bitcast(I32))
-        x_raw1 = load_rows("x_raw1", x, 1)
-        wvd_raw1 = load_rows("wvd_raw1", wvd, 1)
+        load_scale_rows(wv4_plane, wv4_scales)
+        wvd_raw = load_rows("wvd_raw", wvd)
 
-        def interleave(name, engine, raw, c0, width):
-            grouped = tile(name, [P, width, PACK], BF16)
+        def interleave(name, engine, raw, c0, width, tag=None):
+            grouped = tile(name, [P, width, PACK], BF16, tag)
             dst = grouped[:].rearrange("p (c e) i -> p c i e", e=4)
             src = raw[:, :, c0 : c0 + width].rearrange("p i (c e) -> p c i e", e=4)
             if engine == "scalar":
@@ -76,12 +71,10 @@ def tile_list_mlat_dl_scale_kernel(tc, x, w8_words, w8_scales, tab_words, tab_sc
                 nc.vector.tensor_copy(out=dst, in_=src)
             return grouped
 
-        def quantize(name, grouped, tag=None):
-            width = grouped.shape[1]
-            codes = tile(name + "_codes", [P, width], U32, tag)
-            plane = tile(name + "_plane", [P, width], U8)
-            nc.vector.quantize_mx(out=codes[:].bitcast(FP8X4), scales=plane[:], in_=grouped[:].rearrange("p c i -> p (c i)"))
-            return codes, plane
+        def quantize(name, grouped, plane):
+            codes = tile(name + "_codes", [P, grouped.shape[1]], U32)
+            nc.vector.quantize_mx(out=codes[:].bitcast(FP8X4), scales=plane, in_=grouped[:].rearrange("p c i -> p (c i)"))
+            return codes
 
         def gather(name, window, dtype, half, tag=None):
             picked = tile(name, [P, BANK], dtype, tag)
@@ -89,88 +82,78 @@ def tile_list_mlat_dl_scale_kernel(tc, x, w8_words, w8_scales, tab_words, tab_sc
             nc.vector.tensor_copy(picked[:], window[:].indirect(offsets[:, half * cols : (half + 1) * cols]))
             return picked
 
-        xg01 = interleave("x_grouped01", "scalar", x_raw0, 0, HALF)
-        v_plane = [gather("v_plane%d" % h, tab_plane, U8, h) for h in range(2)]
+        def second_plane(plane, t):
+            return plane[4:P, t * P : (t + 1) * P]
+
         w8_codes = tile("w8_codes", [P, R], I32)
         nc.vector.tensor_copy(
             out=w8_codes[:].rearrange("p (i c e) -> p c i e", i=PACK, e=4),
             in_=w8_raw[:].rearrange("p (c e i) -> p c i e", i=PACK, e=4),
         )
-        xq01 = quantize("x01", xg01, "tab_plane")
+        v_plane = [gather("v_plane%d" % h, tab_plane, U8, h) for h in range(2)]
         w8_sorted = tile("w8_sorted", [P, R], U8)
         nc.vector.tensor_copy(
             out=w8_sorted[:].rearrange("p (i c e) -> p c i e", i=PACK, e=16),
             in_=w8_plane[:].rearrange("p (c e i) -> p c i e", i=PACK, e=16),
         )
-        v_codes = [gather("v_codes0", tab_codes, U32, 0, "w8_plane")]
+        xg = [interleave("x_grouped%d" % mt, "scalar", x_raw, mt * P, P) for mt in range(3)]
+        xq = [quantize("x0", xg[0], second_plane(w8_plane, 0))]
+        xg.append(interleave("x_grouped3", "vector", x_raw, 3 * P, P, "x_grouped0"))
+        xq = xq + [quantize("x%d" % mt, xg[mt], second_plane(w8_plane, mt)) for mt in (1, 2, 3)]
 
-        def project(mt, xq, c0, engine):
-            codes, plane = xq
+        def project(mt):
             bank = psum_q.tile([P, PACK, P], F32, name="qa_bank")
             for i in range(PACK):
                 cols = slice(i * P, (i + 1) * P)
                 nc.tensor.matmul_mx(
                     out=bank[:, i, :], lhsT=w8_codes[:, cols].bitcast(FP8X4), lhsT_scale=w8_sorted[:, cols],
-                    rhs=codes[:, c0 : c0 + P].bitcast(FP8X4), rhs_scale=plane[:, c0 : c0 + P], start=True, stop=True,
+                    rhs=xq[mt][:].bitcast(FP8X4), rhs_scale=second_plane(w8_plane, mt), start=True, stop=True,
                 )
             grouped = tile("qa_grouped%d" % mt, [P, P, PACK], BF16)
-            src = bank[:].rearrange("p i m -> p m i")
-            if engine == "scalar":
-                nc.scalar.copy(out=grouped[:], in_=src)
-            else:
-                nc.vector.tensor_copy(out=grouped[:], in_=src)
+            nc.scalar.copy(out=grouped[:], in_=bank[:].rearrange("p i m -> p m i"))
             return grouped
 
-        def store(bank, dst, engine, scale):
-            result = outs.tile([P, BANK], F32, name="result")
-            if engine == "scalar":
-                nc.scalar.activation(out=result[:], in_=bank[:], func=COPY, scale=scale)
-            else:
-                nc.vector.tensor_scalar(out=result[:], in0=bank[:], scalar1=scale, scalar2=None, op0=MULT)
-            nc.sync.dma_start(out=dst, in_=result[:])
+        qg = [project(mt) for mt in range(4)]
+        v_codes = [gather("v_codes0", tab_codes, U32, 0)]
+        qa = [quantize("qa%d" % mt, qg[mt], second_plane(wv4_plane, mt)) for mt in range(3)]
+        v_codes.append(gather("v_codes1", tab_codes, U32, 1, "qa_grouped2"))
+        qa.append(quantize("qa3", qg[3], second_plane(wv4_plane, 3)))
 
-        def scores(mt, qa, h, engine):
-            codes, plane = qa
+        def scores(mt, h):
             bank = psum_o.tile([P, BANK], F32, name="out_bank")
             nc.tensor.matmul_mx(
-                out=bank[:], lhsT=codes[:].bitcast(FP8X4), lhsT_scale=plane[:],
+                out=bank[:], lhsT=qa[mt][:].bitcast(FP8X4), lhsT_scale=second_plane(wv4_plane, mt),
                 rhs=v_codes[h][:].bitcast(FP8X4), rhs_scale=v_plane[h][:], start=True, stop=True,
             )
-            store(bank, out_0[mt * P : (mt + 1) * P, h * BANK : (h + 1) * BANK], engine, SCORE_SCALE)
+            result = tile("scores%d_%d" % (mt, h), [P, BANK], F32)
+            nc.scalar.activation(out=result[:], in_=bank[:], func=COPY, scale=SCORE_SCALE)
+            nc.sync.dma_start(out=out_0[mt * P : (mt + 1) * P, h * BANK : (h + 1) * BANK], in_=result[:])
 
-        def values(nt, wq, c0, h, engine):
-            codes, plane = wq
-            bank = psum_o.tile([P, BANK], F32, name="out_bank")
-            nc.tensor.matmul_mx(
-                out=bank[:], lhsT=codes[:, c0 : c0 + P].bitcast(FP8X4), lhsT_scale=plane[:, c0 : c0 + P],
-                rhs=v_codes[h][:].bitcast(FP8X4), rhs_scale=v_plane[h][:], start=True, stop=False,
-            )
-            nc.tensor.matmul_mx(
-                out=bank[:], lhsT=wv4_codes[:, 2 * nt * P : 2 * (nt + 1) * P].bitcast(FP4X4),
-                lhsT_scale=wv4_plane[:, nt * P : (nt + 1) * P],
-                rhs=v_codes[h][:].bitcast(FP8X4), rhs_scale=v_plane[h][:], start=False, stop=True,
-            )
-            store(bank, out_1[nt * P : (nt + 1) * P, h * BANK : (h + 1) * BANK], engine, 1.0)
+        for mt in range(4):
+            scores(mt, 0)
+        wg = [interleave("wvd_grouped%d" % g, "vector", wvd_raw, g * HALF, HALF) for g in range(2)]
+        wvd_plane = [tile("wvd_plane%d" % g, [P, HALF], U8) for g in range(2)]
+        wvd_codes = [quantize("wvd%d" % g, wg[g], wvd_plane[g][:]) for g in range(2)]
+        for mt in range(4):
+            scores(mt, 1)
 
-        qg = [project(mt, xq01, mt * P, "scalar") for mt in range(2)]
-        wg01 = interleave("wvd_grouped01", "vector", wvd_raw0, 0, HALF)
-        qa = [quantize("qa0", qg[0])]
-        wq01 = quantize("wvd01", wg01)
-        qa.append(quantize("qa1", qg[1]))
-        v_codes.append(gather("v_codes1", tab_codes, U32, 1, "qa_grouped1"))
-        for h in range(2):
-            for t in range(2):
-                scores(t, qa[t], h, "scalar")
-                values(t, wq01, t * P, h, "scalar")
-        xg23 = interleave("x_grouped23", "vector", x_raw1, 0, HALF)
-        wg23 = interleave("wvd_grouped23", "vector", wvd_raw1, 0, HALF)
-        xq23 = quantize("x23", xg23)
-        wq23 = quantize("wvd23", wg23)
-        qg = qg + [project(mt, xq23, (mt - 2) * P, "vector") for mt in (2, 3)]
-        qa = qa + [quantize("qa%d" % mt, qg[mt]) for mt in (2, 3)]
-        for t in (2, 3):
-            values(t, wq23, (t - 2) * P, 0, "scalar")
-            values(t, wq23, (t - 2) * P, 1, "vector")
-        for t in (2, 3):
-            scores(t, qa[t], 0, "vector")
-            scores(t, qa[t], 1, "scalar")
+        for nt in range(4):
+            g, cols = nt // 2, slice(nt % 2 * P, (nt % 2 + 1) * P)
+            result = tile("values%d" % nt, [P, J], F32)
+            for h in range(2):
+                bank = psum_o.tile([P, BANK], F32, name="out_bank")
+                nc.tensor.matmul_mx(
+                    out=bank[:], lhsT=wvd_codes[g][:, cols].bitcast(FP8X4), lhsT_scale=wvd_plane[g][:, cols],
+                    rhs=v_codes[h][:].bitcast(FP8X4), rhs_scale=v_plane[h][:], start=True, stop=False,
+                )
+                nc.tensor.matmul_mx(
+                    out=bank[:], lhsT=wv4_codes[:, 2 * nt * P : 2 * (nt + 1) * P].bitcast(FP4X4),
+                    lhsT_scale=wv4_plane[:, nt * P : (nt + 1) * P],
+                    rhs=v_codes[h][:].bitcast(FP8X4), rhs_scale=v_plane[h][:], start=False, stop=True,
+                )
+                half = result[:, h * BANK : (h + 1) * BANK]
+                if h == 0 or nt == 0:
+                    nc.vector.tensor_copy(out=half, in_=bank[:])
+                else:
+                    nc.scalar.copy(out=half, in_=bank[:])
+            nc.sync.dma_start(out=out_1[nt * P : (nt + 1) * P, :], in_=result[:])

@@ -14,6 +14,7 @@ U8 = mybir.dt.uint8
 FP8X4 = mybir.dt.float8_e4m3fn_x4
 FP4X4 = mybir.dt.float4_e2m1fn_x4
 COPY = mybir.ActivationFunctionType.Copy
+MULT = mybir.AluOpType.mult
 
 P = 128
 PACK = 4
@@ -41,25 +42,30 @@ def tile_list_mlat_dl_scale_kernel(tc, x, w8_words, w8_scales, tab_words, tab_sc
             nc.sync.dma_start(out=raw[:], in_=src.rearrange("(p i) c -> p i c", i=PACK))
             return raw
 
-        tab_plane = tile("tab_plane", [P, T], U8)
+        tab_rows = tile("tab_rows", [P, T], U8)
+        v_plane = tile("v_plane", [P, J], U8)
         w8_plane = tile("w8_plane", [P, R], U8)
         wv4_plane = tile("wv4_plane", [P, N], U8)
-        for plane in (tab_plane, w8_plane, wv4_plane):
+        for plane in (tab_rows, w8_plane, wv4_plane, v_plane):
             nc.vector.memset(plane[:].bitcast(I32), 0)
 
         offsets = keep.tile([P, J // 16], U16, name="offsets")
         nc.sync.dma_start(offsets[:], offs)
         w8_raw = tile("w8_raw", [P, R], I32)
         nc.sync.dma_start(out=w8_raw[:], in_=w8_words[0].rearrange("p r i -> p (r i)").bitcast(I32))
-        load_scale_rows(tab_plane, tab_scales)
+        nc.sync.dma_start(out=tab_rows[0:P:8, :].bitcast(I32), in_=tab_scales[0].bitcast(I32))
         x_raw = load_rows("x_raw", x)
         load_scale_rows(w8_plane, w8_scales)
         tab_codes = tile("tab_codes", [P, T], U32)
         nc.sync.dma_start(out=tab_codes[:].bitcast(I32), in_=tab_words[0].rearrange("p t i -> p (t i)").bitcast(I32))
+        v_rows = tile("v_rows", [P, J], U8)
+        nc.vector.tensor_copy(v_rows[:], tab_rows[:].indirect(offsets[:]))
+        for q in range(4):
+            nc.sync.dma_start(out=v_plane[32 * q : 32 * q + 4, :].bitcast(I32), in_=v_rows[32 * q : 32 * q + 32 : 8, :].bitcast(I32))
+        wvd_raw = load_rows("wvd_raw", wvd)
         wv4_codes = tile("wv4_codes", [P, 2 * N], U8)
         nc.sync.dma_start(out=wv4_codes[:].bitcast(I32), in_=wv4_words[0].bitcast(I32))
         load_scale_rows(wv4_plane, wv4_scales)
-        wvd_raw = load_rows("wvd_raw", wvd)
 
         def interleave(name, engine, raw, c0, width, tag=None):
             grouped = tile(name, [P, width, PACK], BF16, tag)
@@ -90,7 +96,6 @@ def tile_list_mlat_dl_scale_kernel(tc, x, w8_words, w8_scales, tab_words, tab_sc
             out=w8_codes[:].rearrange("p (i c e) -> p c i e", i=PACK, e=4),
             in_=w8_raw[:].rearrange("p (c e i) -> p c i e", i=PACK, e=4),
         )
-        v_plane = [gather("v_plane%d" % h, tab_plane, U8, h) for h in range(2)]
         w8_sorted = tile("w8_sorted", [P, R], U8)
         nc.vector.tensor_copy(
             out=w8_sorted[:].rearrange("p (i c e) -> p c i e", i=PACK, e=16),
@@ -115,27 +120,37 @@ def tile_list_mlat_dl_scale_kernel(tc, x, w8_words, w8_scales, tab_words, tab_sc
 
         qg = [project(mt) for mt in range(4)]
         v_codes = [gather("v_codes0", tab_codes, U32, 0)]
-        qa = [quantize("qa%d" % mt, qg[mt], second_plane(wv4_plane, mt)) for mt in range(3)]
+        qa = [quantize("qa%d" % mt, qg[mt], second_plane(v_plane, 4 + mt)) for mt in range(3)]
         v_codes.append(gather("v_codes1", tab_codes, U32, 1, "qa_grouped2"))
-        qa.append(quantize("qa3", qg[3], second_plane(wv4_plane, 3)))
+        qa.append(quantize("qa3", qg[3], second_plane(v_plane, 4 + 3)))
 
-        def scores(mt, h):
+        def scores(mt, h, result):
             bank = psum_o.tile([P, BANK], F32, name="out_bank")
             nc.tensor.matmul_mx(
-                out=bank[:], lhsT=qa[mt][:].bitcast(FP8X4), lhsT_scale=second_plane(wv4_plane, mt),
-                rhs=v_codes[h][:].bitcast(FP8X4), rhs_scale=v_plane[h][:], start=True, stop=True,
+                out=bank[:], lhsT=qa[mt][:].bitcast(FP8X4), lhsT_scale=second_plane(v_plane, 4 + mt),
+                rhs=v_codes[h][:].bitcast(FP8X4), rhs_scale=v_plane[:, h * BANK : (h + 1) * BANK], start=True, stop=True,
             )
+            if mt == 3 and h == 1:
+                nc.vector.tensor_scalar(out=result, in0=bank[:], scalar1=SCORE_SCALE, scalar2=None, op0=MULT)
+            else:
+                nc.scalar.activation(out=result, in_=bank[:], func=COPY, scale=SCORE_SCALE)
+
+        def scores_half(mt, h):
             result = tile("scores%d_%d" % (mt, h), [P, BANK], F32)
-            nc.scalar.activation(out=result[:], in_=bank[:], func=COPY, scale=SCORE_SCALE)
+            scores(mt, h, result[:])
             nc.sync.dma_start(out=out_0[mt * P : (mt + 1) * P, h * BANK : (h + 1) * BANK], in_=result[:])
 
-        for mt in range(4):
-            scores(mt, 0)
+        for mt in range(3):
+            scores_half(mt, 0)
         wg = [interleave("wvd_grouped%d" % g, "vector", wvd_raw, g * HALF, HALF) for g in range(2)]
         wvd_plane = [tile("wvd_plane%d" % g, [P, HALF], U8) for g in range(2)]
         wvd_codes = [quantize("wvd%d" % g, wg[g], wvd_plane[g][:]) for g in range(2)]
-        for mt in range(4):
-            scores(mt, 1)
+        for mt in range(3):
+            scores_half(mt, 1)
+        last_scores = tile("scores3", [P, J], F32)
+        for h in range(2):
+            scores(3, h, last_scores[:, h * BANK : (h + 1) * BANK])
+        nc.sync.dma_start(out=out_0[3 * P : 4 * P, :], in_=last_scores[:])
 
         for nt in range(4):
             g, cols = nt // 2, slice(nt % 2 * P, (nt % 2 + 1) * P)
@@ -143,16 +158,16 @@ def tile_list_mlat_dl_scale_kernel(tc, x, w8_words, w8_scales, tab_words, tab_sc
             for h in range(2):
                 bank = psum_o.tile([P, BANK], F32, name="out_bank")
                 nc.tensor.matmul_mx(
-                    out=bank[:], lhsT=wvd_codes[g][:, cols].bitcast(FP8X4), lhsT_scale=wvd_plane[g][:, cols],
-                    rhs=v_codes[h][:].bitcast(FP8X4), rhs_scale=v_plane[h][:], start=True, stop=False,
-                )
-                nc.tensor.matmul_mx(
                     out=bank[:], lhsT=wv4_codes[:, 2 * nt * P : 2 * (nt + 1) * P].bitcast(FP4X4),
                     lhsT_scale=wv4_plane[:, nt * P : (nt + 1) * P],
-                    rhs=v_codes[h][:].bitcast(FP8X4), rhs_scale=v_plane[h][:], start=False, stop=True,
+                    rhs=v_codes[h][:].bitcast(FP8X4), rhs_scale=v_plane[:, h * BANK : (h + 1) * BANK], start=True, stop=False,
+                )
+                nc.tensor.matmul_mx(
+                    out=bank[:], lhsT=wvd_codes[g][:, cols].bitcast(FP8X4), lhsT_scale=wvd_plane[g][:, cols],
+                    rhs=v_codes[h][:].bitcast(FP8X4), rhs_scale=v_plane[:, h * BANK : (h + 1) * BANK], start=False, stop=True,
                 )
                 half = result[:, h * BANK : (h + 1) * BANK]
-                if h == 0 or nt == 0:
+                if h == 1:
                     nc.vector.tensor_copy(out=half, in_=bank[:])
                 else:
                     nc.scalar.copy(out=half, in_=bank[:])

@@ -18,8 +18,13 @@ MULT = mybir.AluOpType.mult
 
 P = 128
 PACK = 4
+BLOCKS = 16
+QUADRANT = 32
+LOWER = 4
 BANK = 512
-HALF = 256
+BANKS = 8
+TILES = 4
+WVD_PART = 256
 SCORE_SCALE = 0.03125
 
 
@@ -27,15 +32,19 @@ def tile_list_mlat_dl_scale_kernel(tc, x, w8_words, w8_scales, tab_words, tab_sc
     nc = tc.nc
     with ExitStack() as ctx:
         keep = ctx.enter_context(tc.tile_pool(name="keep", bufs=1))
-        psum_q = ctx.enter_context(tc.psum_pool(name="psum_q", bufs=3))
-        psum_o = ctx.enter_context(tc.psum_pool(name="psum_o", bufs=5))
+        psum = ctx.enter_context(tc.psum_pool(name="psum", bufs=1))
+        banks_used = []
 
-        def tile(name, shape, dtype, tag=None):
-            return keep.tile(shape, dtype, name=name, tag=tag or name, align_bytes=64)
+        def next_bank(shape):
+            banks_used.append(len(banks_used) % BANKS)
+            return psum.tile(shape, F32, name="bank%d" % banks_used[-1])
+
+        def tile(name, shape, dtype, after=None):
+            return keep.tile(shape, dtype, name=name, tag=after or name, align_bytes=64)
 
         def load_scale_rows(plane, rows):
-            for q in range(4):
-                nc.sync.dma_start(out=plane[32 * q : 32 * q + 4, :].bitcast(I32), in_=rows[0, 4 * q : 4 * q + 4, :].bitcast(I32))
+            for r in range(4):
+                nc.sync.dma_start(out=plane[r:P:QUADRANT, :].bitcast(I32), in_=rows[0, r:BLOCKS:4, :].bitcast(I32))
 
         def load_rows(name, src):
             raw = tile(name, [P, PACK, src.shape[1]], F32)
@@ -46,8 +55,8 @@ def tile_list_mlat_dl_scale_kernel(tc, x, w8_words, w8_scales, tab_words, tab_sc
         v_plane = tile("v_plane", [P, J], U8)
         w8_plane = tile("w8_plane", [P, R], U8)
         wv4_plane = tile("wv4_plane", [P, N], U8)
-        for plane in (tab_rows, w8_plane, wv4_plane, v_plane):
-            nc.vector.memset(plane[:].bitcast(I32), 0)
+        for cleared in (tab_rows, w8_plane, wv4_plane, v_plane):
+            nc.vector.memset(cleared[:].bitcast(I32), 0)
 
         offsets = keep.tile([P, J // 16], U16, name="offsets")
         nc.sync.dma_start(offsets[:], offs)
@@ -60,15 +69,15 @@ def tile_list_mlat_dl_scale_kernel(tc, x, w8_words, w8_scales, tab_words, tab_sc
         nc.sync.dma_start(out=tab_codes[:].bitcast(I32), in_=tab_words[0].rearrange("p t i -> p (t i)").bitcast(I32))
         v_rows = tile("v_rows", [P, J], U8)
         nc.vector.tensor_copy(v_rows[:], tab_rows[:].indirect(offsets[:]))
-        for q in range(4):
-            nc.sync.dma_start(out=v_plane[32 * q : 32 * q + 4, :].bitcast(I32), in_=v_rows[32 * q : 32 * q + 32 : 8, :].bitcast(I32))
+        for r in range(4):
+            nc.sync.dma_start(out=v_plane[r:P:QUADRANT, :].bitcast(I32), in_=v_rows[8 * r : P : QUADRANT, :].bitcast(I32))
         wvd_raw = load_rows("wvd_raw", wvd)
         wv4_codes = tile("wv4_codes", [P, 2 * N], U8)
         nc.sync.dma_start(out=wv4_codes[:].bitcast(I32), in_=wv4_words[0].bitcast(I32))
         load_scale_rows(wv4_plane, wv4_scales)
 
-        def interleave(name, engine, raw, c0, width, tag=None):
-            grouped = tile(name, [P, width, PACK], BF16, tag)
+        def interleave(name, engine, raw, c0, width, after=None):
+            grouped = tile(name, [P, width, PACK], BF16, after)
             dst = grouped[:].rearrange("p (c e) i -> p c i e", e=4)
             src = raw[:, :, c0 : c0 + width].rearrange("p i (c e) -> p c i e", e=4)
             if engine == "scalar":
@@ -82,14 +91,17 @@ def tile_list_mlat_dl_scale_kernel(tc, x, w8_words, w8_scales, tab_words, tab_sc
             nc.vector.quantize_mx(out=codes[:].bitcast(FP8X4), scales=plane, in_=grouped[:].rearrange("p c i -> p (c i)"))
             return codes
 
-        def gather(name, window, dtype, half, tag=None):
-            picked = tile(name, [P, BANK], dtype, tag)
-            cols = BANK // 16
-            nc.vector.tensor_copy(picked[:], window[:].indirect(offsets[:, half * cols : (half + 1) * cols]))
+        def gather_words(h, after=None):
+            picked = tile("v_codes%d" % h, [P, BANK], U32, after)
+            list_cols = BANK // 16
+            nc.vector.tensor_copy(picked[:], tab_codes[:].indirect(offsets[:, h * list_cols : (h + 1) * list_cols]))
             return picked
 
-        def second_plane(plane, t):
-            return plane[4:P, t * P : (t + 1) * P]
+        def lower_plane(shared, t):
+            return shared[LOWER:P, t * P : (t + 1) * P]
+
+        def half(h):
+            return slice(h * BANK, (h + 1) * BANK)
 
         w8_codes = tile("w8_codes", [P, R], I32)
         nc.vector.tensor_copy(
@@ -101,74 +113,86 @@ def tile_list_mlat_dl_scale_kernel(tc, x, w8_words, w8_scales, tab_words, tab_sc
             out=w8_sorted[:].rearrange("p (i c e) -> p c i e", i=PACK, e=16),
             in_=w8_plane[:].rearrange("p (c e i) -> p c i e", i=PACK, e=16),
         )
-        xg = [interleave("x_grouped%d" % mt, "scalar", x_raw, mt * P, P) for mt in range(3)]
-        xq = [quantize("x0", xg[0], second_plane(w8_plane, 0))]
-        xg.append(interleave("x_grouped3", "vector", x_raw, 3 * P, P, "x_grouped0"))
-        xq = xq + [quantize("x%d" % mt, xg[mt], second_plane(w8_plane, mt)) for mt in (1, 2, 3)]
+
+        x_plane = [lower_plane(w8_plane, mt) for mt in range(TILES)]
+        x_grouped = [interleave("x_grouped%d" % mt, "scalar", x_raw, mt * P, P) for mt in range(TILES - 1)]
+        x_codes = [quantize("x0", x_grouped[0], x_plane[0])]
+        x_grouped.append(interleave("x_grouped3", "vector", x_raw, (TILES - 1) * P, P, after="x_grouped0"))
+        x_codes = x_codes + [quantize("x%d" % mt, x_grouped[mt], x_plane[mt]) for mt in range(1, TILES)]
 
         def project(mt):
-            bank = psum_q.tile([P, PACK, P], F32, name="qa_bank")
+            bank = next_bank([P, PACK, P])
             for i in range(PACK):
                 cols = slice(i * P, (i + 1) * P)
                 nc.tensor.matmul_mx(
                     out=bank[:, i, :], lhsT=w8_codes[:, cols].bitcast(FP8X4), lhsT_scale=w8_sorted[:, cols],
-                    rhs=xq[mt][:].bitcast(FP8X4), rhs_scale=second_plane(w8_plane, mt), start=True, stop=True,
+                    rhs=x_codes[mt][:].bitcast(FP8X4), rhs_scale=x_plane[mt], start=True, stop=True,
                 )
             grouped = tile("qa_grouped%d" % mt, [P, P, PACK], BF16)
             nc.scalar.copy(out=grouped[:], in_=bank[:].rearrange("p i m -> p m i"))
             return grouped
 
-        qg = [project(mt) for mt in range(4)]
-        v_codes = [gather("v_codes0", tab_codes, U32, 0)]
-        qa = [quantize("qa%d" % mt, qg[mt], second_plane(v_plane, 4 + mt)) for mt in range(3)]
-        v_codes.append(gather("v_codes1", tab_codes, U32, 1, "qa_grouped2"))
-        qa.append(quantize("qa3", qg[3], second_plane(v_plane, 4 + 3)))
+        qa_grouped = [project(mt) for mt in range(TILES)]
 
-        def scores(mt, h, result):
-            bank = psum_o.tile([P, BANK], F32, name="out_bank")
+        under_second_half = BANK // P
+        qa_plane = [lower_plane(v_plane, t) for t in (under_second_half, under_second_half + 1, 0, 1)]
+        v_codes = [gather_words(0)]
+        qa_codes = [quantize("qa%d" % mt, qa_grouped[mt], qa_plane[mt]) for mt in (0, 1)]
+        v_codes.append(gather_words(1, after="qa_grouped0"))
+
+        def scores(mt, h, result, engine):
+            bank = next_bank([P, BANK])
             nc.tensor.matmul_mx(
-                out=bank[:], lhsT=qa[mt][:].bitcast(FP8X4), lhsT_scale=second_plane(v_plane, 4 + mt),
-                rhs=v_codes[h][:].bitcast(FP8X4), rhs_scale=v_plane[:, h * BANK : (h + 1) * BANK], start=True, stop=True,
+                out=bank[:], lhsT=qa_codes[mt][:].bitcast(FP8X4), lhsT_scale=qa_plane[mt],
+                rhs=v_codes[h][:].bitcast(FP8X4), rhs_scale=v_plane[:, half(h)], start=True, stop=True,
             )
-            if mt == 3 and h == 1:
-                nc.vector.tensor_scalar(out=result, in0=bank[:], scalar1=SCORE_SCALE, scalar2=None, op0=MULT)
-            else:
+            if engine == "scalar":
                 nc.scalar.activation(out=result, in_=bank[:], func=COPY, scale=SCORE_SCALE)
+            else:
+                nc.vector.tensor_scalar(out=result, in0=bank[:], scalar1=SCORE_SCALE, scalar2=None, op0=MULT)
 
         def scores_half(mt, h):
             result = tile("scores%d_%d" % (mt, h), [P, BANK], F32)
-            scores(mt, h, result[:])
-            nc.sync.dma_start(out=out_0[mt * P : (mt + 1) * P, h * BANK : (h + 1) * BANK], in_=result[:])
+            scores(mt, h, result[:], "scalar")
+            nc.sync.dma_start(out=out_0[mt * P : (mt + 1) * P, half(h)], in_=result[:])
 
-        for mt in range(3):
+        def scores_whole(mt, after):
+            result = tile("scores%d" % mt, [P, J], F32, after)
+            scores(mt, 0, result[:, half(0)], "scalar")
+            scores(mt, 1, result[:, half(1)], "vector")
+            nc.sync.dma_start(out=out_0[mt * P : (mt + 1) * P, :], in_=result[:])
+
+        for mt in (0, 1):
             scores_half(mt, 0)
-        wg = [interleave("wvd_grouped%d" % g, "vector", wvd_raw, g * HALF, HALF) for g in range(2)]
-        wvd_plane = [tile("wvd_plane%d" % g, [P, HALF], U8) for g in range(2)]
-        wvd_codes = [quantize("wvd%d" % g, wg[g], wvd_plane[g][:]) for g in range(2)]
-        for mt in range(3):
+        qa_codes = qa_codes + [quantize("qa%d" % mt, qa_grouped[mt], qa_plane[mt]) for mt in (2, 3)]
+        for mt in (0, 1):
             scores_half(mt, 1)
-        last_scores = tile("scores3", [P, J], F32)
-        for h in range(2):
-            scores(3, h, last_scores[:, h * BANK : (h + 1) * BANK])
-        nc.sync.dma_start(out=out_0[3 * P : 4 * P, :], in_=last_scores[:])
 
-        for nt in range(4):
-            g, cols = nt // 2, slice(nt % 2 * P, (nt % 2 + 1) * P)
+        parts = N // WVD_PART
+        wvd_plane = [tile("wvd_plane%d" % g, [P, WVD_PART], U8) for g in range(parts)]
+        wvd_grouped = [interleave("wvd_grouped%d" % g, "vector", wvd_raw, g * WVD_PART, WVD_PART) for g in range(parts)]
+        wvd_codes = [quantize("wvd0", wvd_grouped[0], wvd_plane[0][:])]
+        scores_whole(2, after="wvd_raw")
+        wvd_codes.append(quantize("wvd1", wvd_grouped[1], wvd_plane[1][:]))
+        scores_whole(3, after="wvd_grouped0")
+
+        for nt in range(TILES):
+            g, c0 = divmod(nt * P, WVD_PART)
+            wvd_cols = slice(c0, c0 + P)
             result = tile("values%d" % nt, [P, J], F32)
             for h in range(2):
-                bank = psum_o.tile([P, BANK], F32, name="out_bank")
+                bank = next_bank([P, BANK])
                 nc.tensor.matmul_mx(
                     out=bank[:], lhsT=wv4_codes[:, 2 * nt * P : 2 * (nt + 1) * P].bitcast(FP4X4),
                     lhsT_scale=wv4_plane[:, nt * P : (nt + 1) * P],
-                    rhs=v_codes[h][:].bitcast(FP8X4), rhs_scale=v_plane[:, h * BANK : (h + 1) * BANK], start=True, stop=False,
+                    rhs=v_codes[h][:].bitcast(FP8X4), rhs_scale=v_plane[:, half(h)], start=True, stop=False,
                 )
                 nc.tensor.matmul_mx(
-                    out=bank[:], lhsT=wvd_codes[g][:, cols].bitcast(FP8X4), lhsT_scale=wvd_plane[g][:, cols],
-                    rhs=v_codes[h][:].bitcast(FP8X4), rhs_scale=v_plane[:, h * BANK : (h + 1) * BANK], start=False, stop=True,
+                    out=bank[:], lhsT=wvd_codes[g][:, wvd_cols].bitcast(FP8X4), lhsT_scale=wvd_plane[g][:, wvd_cols],
+                    rhs=v_codes[h][:].bitcast(FP8X4), rhs_scale=v_plane[:, half(h)], start=False, stop=True,
                 )
-                half = result[:, h * BANK : (h + 1) * BANK]
-                if h == 1:
-                    nc.vector.tensor_copy(out=half, in_=bank[:])
+                if h == 0:
+                    nc.scalar.copy(out=result[:, half(h)], in_=bank[:])
                 else:
-                    nc.scalar.copy(out=half, in_=bank[:])
+                    nc.vector.tensor_copy(out=result[:, half(h)], in_=bank[:])
             nc.sync.dma_start(out=out_1[nt * P : (nt + 1) * P, :], in_=result[:])

@@ -26,6 +26,7 @@ BANKS = 8
 TILES = 4
 WVD_PART = 256
 SCORE_SCALE = 0.03125
+W8_FIRST = 12
 
 
 def tile_list_mlat_dl_scale_kernel(tc, x, w8_words, w8_scales, tab_words, tab_scales, wv4_words, wv4_scales, wvd, offs, out_0, out_1):
@@ -42,9 +43,9 @@ def tile_list_mlat_dl_scale_kernel(tc, x, w8_words, w8_scales, tab_words, tab_sc
         def tile(name, shape, dtype, after=None):
             return keep.tile(shape, dtype, name=name, tag=after or name, align_bytes=64)
 
-        def load_scale_rows(plane, rows):
+        def load_scale_rows(plane, rows, first):
             for r in range(4):
-                nc.sync.dma_start(out=plane[r:P:QUADRANT, :].bitcast(I32), in_=rows[0, r:BLOCKS:4, :].bitcast(I32))
+                nc.sync.dma_start(out=plane[first + r : P : QUADRANT, :].bitcast(I32), in_=rows[0, r:BLOCKS:4, :].bitcast(I32))
 
         def load_rows(name, src):
             raw = tile(name, [P, PACK, src.shape[1]], F32)
@@ -58,13 +59,13 @@ def tile_list_mlat_dl_scale_kernel(tc, x, w8_words, w8_scales, tab_words, tab_sc
         for cleared in (tab_rows, w8_plane, wv4_plane, v_plane):
             nc.vector.memset(cleared[:].bitcast(I32), 0)
 
-        offsets = keep.tile([P, J // 16], U16, name="offsets")
-        nc.sync.dma_start(offsets[:], offs)
         w8_raw = tile("w8_raw", [P, R], I32)
         nc.sync.dma_start(out=w8_raw[:], in_=w8_words[0].rearrange("p r i -> p (r i)").bitcast(I32))
+        offsets = keep.tile([P, J // 16], U16, name="offsets")
+        nc.sync.dma_start(offsets[:], offs)
         nc.sync.dma_start(out=tab_rows[0:P:8, :].bitcast(I32), in_=tab_scales[0].bitcast(I32))
         x_raw = load_rows("x_raw", x)
-        load_scale_rows(w8_plane, w8_scales)
+        load_scale_rows(w8_plane, w8_scales, W8_FIRST)
         tab_codes = tile("tab_codes", [P, T], U32)
         nc.sync.dma_start(out=tab_codes[:].bitcast(I32), in_=tab_words[0].rearrange("p t i -> p (t i)").bitcast(I32))
         v_rows = tile("v_rows", [P, J], U8)
@@ -74,7 +75,7 @@ def tile_list_mlat_dl_scale_kernel(tc, x, w8_words, w8_scales, tab_words, tab_sc
         wvd_raw = load_rows("wvd_raw", wvd)
         wv4_codes = tile("wv4_codes", [P, 2 * N], U8)
         nc.sync.dma_start(out=wv4_codes[:].bitcast(I32), in_=wv4_words[0].bitcast(I32))
-        load_scale_rows(wv4_plane, wv4_scales)
+        load_scale_rows(wv4_plane, wv4_scales, 0)
 
         def interleave(name, engine, raw, c0, width, after=None):
             grouped = tile(name, [P, width, PACK], BF16, after)
@@ -114,7 +115,7 @@ def tile_list_mlat_dl_scale_kernel(tc, x, w8_words, w8_scales, tab_words, tab_sc
             in_=w8_plane[:].rearrange("p (c e i) -> p c i e", i=PACK, e=16),
         )
 
-        x_plane = [lower_plane(w8_plane, mt) for mt in range(TILES)]
+        x_plane = [w8_plane[:, mt * P : (mt + 1) * P] for mt in range(TILES)]
         x_grouped = [interleave("x_grouped%d" % mt, "scalar", x_raw, mt * P, P) for mt in range(TILES - 1)]
         x_codes = [quantize("x0", x_grouped[0], x_plane[0])]
         x_grouped.append(interleave("x_grouped3", "vector", x_raw, (TILES - 1) * P, P, after="x_grouped0"))
@@ -125,7 +126,7 @@ def tile_list_mlat_dl_scale_kernel(tc, x, w8_words, w8_scales, tab_words, tab_sc
             for i in range(PACK):
                 cols = slice(i * P, (i + 1) * P)
                 nc.tensor.matmul_mx(
-                    out=bank[:, i, :], lhsT=w8_codes[:, cols].bitcast(FP8X4), lhsT_scale=w8_sorted[:, cols],
+                    out=bank[:, i, :], lhsT=w8_codes[:, cols].bitcast(FP8X4), lhsT_scale=w8_sorted[W8_FIRST:P, cols],
                     rhs=x_codes[mt][:].bitcast(FP8X4), rhs_scale=x_plane[mt], start=True, stop=True,
                 )
             grouped = tile("qa_grouped%d" % mt, [P, P, PACK], BF16)

@@ -23,6 +23,7 @@ QUADRANT = 32
 LOWER = 4
 BANK = 512
 BANKS = 8
+QUARTER = 256
 TILES = 4
 WVD_PART = 256
 SCORE_SCALE = 0.03125
@@ -87,16 +88,18 @@ def tile_list_mlat_dl_scale_kernel(tc, x, w8_words, w8_scales, tab_words, tab_sc
                 nc.vector.tensor_copy(out=dst, in_=src)
             return grouped
 
-        def quantize(name, grouped, plane):
-            codes = tile(name + "_codes", [P, grouped.shape[1]], U32)
+        def quantize(name, grouped, plane, after=None):
+            codes = tile(name + "_codes", [P, grouped.shape[1]], U32, after)
             nc.vector.quantize_mx(out=codes[:].bitcast(FP8X4), scales=plane, in_=grouped[:].rearrange("p c i -> p (c i)"))
             return codes
 
-        def gather_words(h, after=None):
-            picked = tile("v_codes%d" % h, [P, BANK], U32, after)
-            list_cols = BANK // 16
-            nc.vector.tensor_copy(picked[:], tab_codes[:].indirect(offsets[:, h * list_cols : (h + 1) * list_cols]))
-            return picked
+        def gather_words(cols, after=None, parts=1):
+            picked = tile("v_codes%d" % cols.start, [P, cols.stop - cols.start], U32, after)
+            width = (cols.stop - cols.start) // parts
+            for c0 in range(cols.start, cols.stop, width):
+                listed = offsets[:, c0 // 16 : (c0 + width) // 16]
+                nc.vector.tensor_copy(picked[:, c0 - cols.start : c0 - cols.start + width], tab_codes[:].indirect(listed))
+            v_codes[(cols.start, cols.stop)] = picked
 
         def lower_plane(shared, t):
             return shared[LOWER:P, t * P : (t + 1) * P]
@@ -129,71 +132,113 @@ def tile_list_mlat_dl_scale_kernel(tc, x, w8_words, w8_scales, tab_words, tab_sc
                     out=bank[:, i, :], lhsT=w8_codes[:, cols].bitcast(FP8X4), lhsT_scale=w8_sorted[W8_FIRST:P, cols],
                     rhs=x_codes[mt][:].bitcast(FP8X4), rhs_scale=x_plane[mt], start=True, stop=True,
                 )
-            grouped = tile("qa_grouped%d" % mt, [P, P, PACK], BF16)
-            nc.scalar.copy(out=grouped[:], in_=bank[:].rearrange("p i m -> p m i"))
+            return bank
+
+        def leave_bank(mt, bank, engine, after=None):
+            grouped = tile("qa_grouped%d" % mt, [P, P, PACK], BF16, after)
+            if engine == "scalar":
+                nc.scalar.copy(out=grouped[:], in_=bank[:].rearrange("p i m -> p m i"))
+            else:
+                nc.vector.tensor_copy(out=grouped[:], in_=bank[:].rearrange("p i m -> p m i"))
             return grouped
 
-        qa_grouped = [project(mt) for mt in range(TILES)]
+        qa_bank = [project(mt) for mt in range(TILES)]
+        qa_grouped = [leave_bank(mt, qa_bank[mt], "scalar") for mt in range(TILES - 1)]
 
         under_second_half = BANK // P
-        qa_plane = [lower_plane(v_plane, t) for t in (under_second_half, under_second_half + 1, 0, 1)]
-        v_codes = [gather_words(0)]
-        qa_codes = [quantize("qa%d" % mt, qa_grouped[mt], qa_plane[mt]) for mt in (0, 1)]
-        v_codes.append(gather_words(1, after="qa_grouped0"))
+        qa_plane = [lower_plane(v_plane, under_second_half + t) for t in range(TILES - 1)]
+        qa3_plane = tile("qa3_plane", [P, P], U8)
+        qa_plane.append(qa3_plane[:])
+        v_codes = {}
 
-        def scores(mt, h, result, engine):
-            bank = next_bank([P, BANK])
-            nc.tensor.matmul_mx(
-                out=bank[:], lhsT=qa_codes[mt][:].bitcast(FP8X4), lhsT_scale=qa_plane[mt],
-                rhs=v_codes[h][:].bitcast(FP8X4), rhs_scale=v_plane[:, half(h)], start=True, stop=True,
-            )
+        def pieces(cols):
+            found = []
+            for h0, h1 in sorted(v_codes):
+                c0, c1 = max(h0, cols.start), min(h1, cols.stop)
+                if c0 < c1:
+                    found.append(((c0, c1), v_codes[(h0, h1)][:, c0 - h0 : c1 - h0]))
+            return found
+
+        def scores(mt, cols, result, engine):
+            bank = next_bank([P, cols.stop - cols.start])
+            for (c0, c1), codes in pieces(cols):
+                nc.tensor.matmul_mx(
+                    out=bank[:, c0 - cols.start : c1 - cols.start], lhsT=qa_codes[mt][:].bitcast(FP8X4), lhsT_scale=qa_plane[mt],
+                    rhs=codes.bitcast(FP8X4), rhs_scale=v_plane[:, c0:c1], start=True, stop=True,
+                )
             if engine == "scalar":
                 nc.scalar.activation(out=result, in_=bank[:], func=COPY, scale=SCORE_SCALE)
             else:
                 nc.vector.tensor_scalar(out=result, in0=bank[:], scalar1=SCORE_SCALE, scalar2=None, op0=MULT)
 
-        def scores_half(mt, h):
-            result = tile("scores%d_%d" % (mt, h), [P, BANK], F32)
-            scores(mt, h, result[:], "scalar")
-            nc.sync.dma_start(out=out_0[mt * P : (mt + 1) * P, half(h)], in_=result[:])
+        def scores_part(mt, cols, parts=1):
+            result = tile("scores%d_%d" % (mt, cols.start), [P, cols.stop - cols.start], F32)
+            width = (cols.stop - cols.start) // parts
+            for c0 in range(cols.start, cols.stop, width):
+                scores(mt, slice(c0, c0 + width), result[:, c0 - cols.start : c0 - cols.start + width], "scalar")
+            nc.sync.dma_start(out=out_0[mt * P : (mt + 1) * P, cols], in_=result[:])
 
         def scores_whole(mt, after):
             result = tile("scores%d" % mt, [P, J], F32, after)
-            scores(mt, 0, result[:, half(0)], "scalar")
-            scores(mt, 1, result[:, half(1)], "vector")
+            scores(mt, half(0), result[:, half(0)], "scalar")
+            scores(mt, half(1), result[:, half(1)], "vector")
             nc.sync.dma_start(out=out_0[mt * P : (mt + 1) * P, :], in_=result[:])
 
-        for mt in (0, 1):
-            scores_half(mt, 0)
-        qa_codes = qa_codes + [quantize("qa%d" % mt, qa_grouped[mt], qa_plane[mt]) for mt in (2, 3)]
-        for mt in (0, 1):
-            scores_half(mt, 1)
+        quarter = [slice(0, QUARTER), slice(QUARTER, BANK)]
+        gather_words(quarter[0])
+        qa_codes = [quantize("qa0", qa_grouped[0], qa_plane[0])]
+        gather_words(quarter[1], after="v_rows")
+        scores_part(0, quarter[0])
+        qa_codes.append(quantize("qa1", qa_grouped[1], qa_plane[1]))
+        scores_part(0, quarter[1])
+        qa_codes.append(quantize("qa2", qa_grouped[2], qa_plane[2]))
+        gather_words(half(1), after="qa_grouped0", parts=2)
+        for mt in (1, 2):
+            scores_part(mt, half(0))
+        qa_grouped.append(leave_bank(3, qa_bank[3], "vector", after="qa_grouped1"))
+        scores_part(0, half(1), parts=2)
+        for mt in (1, 2):
+            scores_part(mt, half(1))
+        qa_codes.append(quantize("qa3", qa_grouped[3], qa_plane[3]))
 
-        parts = N // WVD_PART
-        wvd_plane = [tile("wvd_plane%d" % g, [P, WVD_PART], U8) for g in range(parts)]
-        wvd_grouped = [interleave("wvd_grouped%d" % g, "vector", wvd_raw, g * WVD_PART, WVD_PART) for g in range(parts)]
-        wvd_codes = [quantize("wvd0", wvd_grouped[0], wvd_plane[0][:])]
-        scores_whole(2, after="wvd_raw")
-        wvd_codes.append(quantize("wvd1", wvd_grouped[1], wvd_plane[1][:]))
+        wvd_part = [(0, P), (P, P), (2 * P, 2 * P)]
+        wvd_plane = [tile("wvd_plane%d" % g, [P, width], U8) for g, (c0, width) in enumerate(wvd_part)]
+        wvd_grouped = [interleave("wvd_grouped%d" % g, "vector", wvd_raw, g * P, P) for g in (0, 1)]
+        wvd_codes = [quantize("wvd%d" % g, wvd_grouped[g], wvd_plane[g][:]) for g in (0, 1)]
         scores_whole(3, after="wvd_grouped0")
+        wvd_grouped.append(interleave("wvd_grouped2", "vector", wvd_raw, 2 * P, 2 * P))
 
-        for nt in range(TILES):
-            g, c0 = divmod(nt * P, WVD_PART)
-            wvd_cols = slice(c0, c0 + P)
+        def values(nt):
+            g = min(nt, 2)
+            w0 = nt * P - wvd_part[g][0]
+            wvd_cols = slice(w0, w0 + P)
             result = tile("values%d" % nt, [P, J], F32)
+            banks = [next_bank([P, BANK]) for h in range(2)]
             for h in range(2):
-                bank = next_bank([P, BANK])
-                nc.tensor.matmul_mx(
-                    out=bank[:], lhsT=wv4_codes[:, 2 * nt * P : 2 * (nt + 1) * P].bitcast(FP4X4),
-                    lhsT_scale=wv4_plane[:, nt * P : (nt + 1) * P],
-                    rhs=v_codes[h][:].bitcast(FP8X4), rhs_scale=v_plane[:, half(h)], start=True, stop=False,
-                )
-                nc.tensor.matmul_mx(
-                    out=bank[:], lhsT=wvd_codes[g][:, wvd_cols].bitcast(FP8X4), lhsT_scale=wvd_plane[g][:, wvd_cols],
-                    rhs=v_codes[h][:].bitcast(FP8X4), rhs_scale=v_plane[:, half(h)], start=False, stop=True,
-                )
-                if h == 0:
-                    nc.scalar.copy(out=result[:, half(h)], in_=bank[:])
-                else:
-                    nc.vector.tensor_copy(out=result[:, half(h)], in_=bank[:])
+                first = True
+                for (c0, c1), codes in pieces(half(h)):
+                    width = BANK if c1 - c0 == BANK else P
+                    for b in range(0, c1 - c0, width):
+                        nc.tensor.matmul_mx(
+                            out=banks[h][:, c0 % BANK + b : c0 % BANK + b + width],
+                            lhsT=wv4_codes[:, 2 * nt * P : 2 * (nt + 1) * P].bitcast(FP4X4),
+                            lhsT_scale=wv4_plane[:, nt * P : (nt + 1) * P],
+                            rhs=codes[:, b : b + width].bitcast(FP8X4), rhs_scale=v_plane[:, c0 + b : c0 + b + width],
+                            start=first, stop=False,
+                        )
+                        first = False
+            for h in range(2):
+                for (c0, c1), codes in pieces(half(h)):
+                    nc.tensor.matmul_mx(
+                        out=banks[h][:, c0 % BANK : c0 % BANK + c1 - c0],
+                        lhsT=wvd_codes[g][:, wvd_cols].bitcast(FP8X4), lhsT_scale=wvd_plane[g][:, wvd_cols],
+                        rhs=codes.bitcast(FP8X4), rhs_scale=v_plane[:, c0:c1], start=False, stop=c1 % BANK == 0,
+                    )
+            nc.scalar.copy(out=result[:, half(0)], in_=banks[0][:])
+            nc.vector.tensor_copy(out=result[:, half(1)], in_=banks[1][:])
             nc.sync.dma_start(out=out_1[nt * P : (nt + 1) * P, :], in_=result[:])
+
+        values(0)
+        wvd_codes.append(quantize("wvd2", wvd_grouped[2], wvd_plane[2][:], after="wvd0_codes"))
+        for nt in range(1, TILES):
+            values(nt)

@@ -23,7 +23,6 @@ QUADRANT = 32
 LOWER = 4
 BANK = 512
 BANKS = 8
-QUARTER = 256
 TILES = 4
 WVD_PART = 256
 SCORE_SCALE = 0.03125
@@ -184,20 +183,13 @@ def tile_list_mlat_dl_scale_kernel(tc, x, w8_words, w8_scales, tab_words, tab_sc
             scores(mt, half(1), result[:, half(1)], "vector")
             nc.sync.dma_start(out=out_0[mt * P : (mt + 1) * P, :], in_=result[:])
 
-        quarter = [slice(0, QUARTER), slice(QUARTER, BANK)]
-        gather_words(quarter[0])
-        qa_codes = [quantize("qa0", qa_grouped[0], qa_plane[0])]
-        gather_words(quarter[1], after="v_rows")
-        scores_part(0, quarter[0])
-        qa_codes.append(quantize("qa1", qa_grouped[1], qa_plane[1]))
-        scores_part(0, quarter[1])
-        qa_codes.append(quantize("qa2", qa_grouped[2], qa_plane[2]))
-        gather_words(half(1), after="qa_grouped0", parts=2)
-        for mt in (1, 2):
+        gather_words(half(0))
+        qa_codes = [quantize("qa%d" % mt, qa_grouped[mt], qa_plane[mt]) for mt in range(TILES - 1)]
+        gather_words(half(1), after="qa_grouped0")
+        for mt in range(TILES - 1):
             scores_part(mt, half(0))
         qa_grouped.append(leave_bank(3, qa_bank[3], "vector", after="qa_grouped1"))
-        scores_part(0, half(1), parts=2)
-        for mt in (1, 2):
+        for mt in range(TILES - 1):
             scores_part(mt, half(1))
         qa_codes.append(quantize("qa3", qa_grouped[3], qa_plane[3]))
 

@@ -26,6 +26,7 @@ BANKS = 8
 TILES = 4
 WVD_PART = 256
 SCORE_SCALE = 0.03125
+EARLY = 3
 W8_FIRST = 12
 
 
@@ -43,9 +44,9 @@ def tile_list_mlat_dl_scale_kernel(tc, x, w8_words, w8_scales, tab_words, tab_sc
         def tile(name, shape, dtype, after=None):
             return keep.tile(shape, dtype, name=name, tag=after or name, align_bytes=64)
 
-        def load_scale_rows(plane, rows, first):
+        def load_scale_rows(plane, rows, first, queues):
             for r in range(4):
-                nc.sync.dma_start(out=plane[first + r : P : QUADRANT, :].bitcast(I32), in_=rows[0, r:BLOCKS:4, :].bitcast(I32))
+                queues[r].dma_start(out=plane[first + r : P : QUADRANT, :].bitcast(I32), in_=rows[0, r:BLOCKS:4, :].bitcast(I32))
 
         def load_rows(name, src):
             raw = tile(name, [P, PACK, src.shape[1]], F32)
@@ -56,18 +57,25 @@ def tile_list_mlat_dl_scale_kernel(tc, x, w8_words, w8_scales, tab_words, tab_sc
         v_plane = tile("v_plane", [P, J], U8)
         w8_plane = tile("w8_plane", [P, R], U8)
         wv4_plane = tile("wv4_plane", [P, N], U8)
-        for cleared in (tab_rows, w8_plane, wv4_plane, v_plane):
+        nc.gpsimd.memset(w8_plane[:].bitcast(I32), 0)
+        for cleared in (tab_rows, wv4_plane, v_plane):
             nc.vector.memset(cleared[:].bitcast(I32), 0)
 
-        w8_raw = tile("w8_raw", [P, R], I32)
-        nc.sync.dma_start(out=w8_raw[:], in_=w8_words[0].rearrange("p r i -> p (r i)").bitcast(I32))
         offsets = keep.tile([P, J // 16], U16, name="offsets")
         nc.sync.dma_start(offsets[:], offs)
+        w8_raw = tile("w8_raw", [P, R], U32)
+        nc.sync.dma_start(out=w8_raw[:].bitcast(I32), in_=w8_words[0].rearrange("p r i -> p (r i)").bitcast(I32))
+        load_scale_rows(w8_plane, w8_scales, W8_FIRST, (nc.sync, nc.sync, nc.scalar, nc.scalar))
         nc.sync.dma_start(out=tab_rows[0:P:8, :].bitcast(I32), in_=tab_scales[0].bitcast(I32))
-        x_raw = load_rows("x_raw", x)
-        load_scale_rows(w8_plane, w8_scales, W8_FIRST)
+        x_early = load_rows("x_early", x[:, 0 : EARLY * P])
         tab_codes = tile("tab_codes", [P, T], U32)
         nc.sync.dma_start(out=tab_codes[:].bitcast(I32), in_=tab_words[0].rearrange("p t i -> p (t i)").bitcast(I32))
+        x_late = load_rows("x_late", x[:, EARLY * P : M])
+        w8_sorted = tile("w8_sorted", [P, R], U8)
+        nc.vector.tensor_copy(
+            out=w8_sorted[:].rearrange("p (i c e) -> p c i e", i=PACK, e=16),
+            in_=w8_plane[:].rearrange("p (c e i) -> p c i e", i=PACK, e=16),
+        )
         v_rows = tile("v_rows", [P, J], U8)
         nc.vector.tensor_copy(v_rows[:], tab_rows[:].indirect(offsets[:]))
         for r in range(4):
@@ -75,7 +83,7 @@ def tile_list_mlat_dl_scale_kernel(tc, x, w8_words, w8_scales, tab_words, tab_sc
         wvd_raw = load_rows("wvd_raw", wvd)
         wv4_codes = tile("wv4_codes", [P, 2 * N], U8)
         nc.sync.dma_start(out=wv4_codes[:].bitcast(I32), in_=wv4_words[0].bitcast(I32))
-        load_scale_rows(wv4_plane, wv4_scales, 0)
+        load_scale_rows(wv4_plane, wv4_scales, 0, (nc.sync,) * 4)
 
         def interleave(name, engine, raw, c0, width, after=None):
             grouped = tile(name, [P, width, PACK], BF16, after)
@@ -89,39 +97,29 @@ def tile_list_mlat_dl_scale_kernel(tc, x, w8_words, w8_scales, tab_words, tab_sc
 
         def quantize(name, grouped, plane, after=None):
             codes = tile(name + "_codes", [P, grouped.shape[1]], U32, after)
-            nc.vector.quantize_mx(out=codes[:].bitcast(FP8X4), scales=plane, in_=grouped[:].rearrange("p c i -> p (c i)"))
+            nc.vector.quantize_mx(out=codes[:].bitcast(FP8X4), scales=plane, in_=grouped[:, :, :].rearrange("p c i -> p (c i)"))
             return codes
-
-        def gather_words(cols, after=None, parts=1):
-            picked = tile("v_codes%d" % cols.start, [P, cols.stop - cols.start], U32, after)
-            width = (cols.stop - cols.start) // parts
-            for c0 in range(cols.start, cols.stop, width):
-                listed = offsets[:, c0 // 16 : (c0 + width) // 16]
-                nc.vector.tensor_copy(picked[:, c0 - cols.start : c0 - cols.start + width], tab_codes[:].indirect(listed))
-            v_codes[(cols.start, cols.stop)] = picked
-
-        def lower_plane(shared, t):
-            return shared[LOWER:P, t * P : (t + 1) * P]
 
         def half(h):
             return slice(h * BANK, (h + 1) * BANK)
 
-        w8_codes = tile("w8_codes", [P, R], I32)
-        nc.vector.tensor_copy(
+        def gather_words(h, after=None):
+            picked = tile("v_codes%d" % h, [P, BANK], U32, after)
+            nc.vector.tensor_copy(picked[:], tab_codes[:].indirect(offsets[:, h * BANK // 16 : (h + 1) * BANK // 16]))
+            return picked
+
+        def lower_plane(shared, t):
+            return shared[LOWER:P, t * P : (t + 1) * P]
+
+        w8_codes = tile("w8_codes", [P, R], U32)
+        nc.scalar.copy(
             out=w8_codes[:].rearrange("p (i c e) -> p c i e", i=PACK, e=4),
             in_=w8_raw[:].rearrange("p (c e i) -> p c i e", i=PACK, e=4),
         )
-        w8_sorted = tile("w8_sorted", [P, R], U8)
-        nc.vector.tensor_copy(
-            out=w8_sorted[:].rearrange("p (i c e) -> p c i e", i=PACK, e=16),
-            in_=w8_plane[:].rearrange("p (c e i) -> p c i e", i=PACK, e=16),
-        )
 
         x_plane = [w8_plane[:, mt * P : (mt + 1) * P] for mt in range(TILES)]
-        x_grouped = [interleave("x_grouped%d" % mt, "scalar", x_raw, mt * P, P) for mt in range(TILES - 1)]
-        x_codes = [quantize("x0", x_grouped[0], x_plane[0])]
-        x_grouped.append(interleave("x_grouped3", "vector", x_raw, (TILES - 1) * P, P, after="x_grouped0"))
-        x_codes = x_codes + [quantize("x%d" % mt, x_grouped[mt], x_plane[mt]) for mt in range(1, TILES)]
+        x_grouped = [interleave("x_grouped%d" % mt, "scalar", x_early, mt * P, P) for mt in range(EARLY)]
+        x_codes = [quantize("x%d" % mt, x_grouped[mt], x_plane[mt]) for mt in range(EARLY)]
 
         def project(mt):
             bank = next_bank([P, PACK, P])
@@ -133,104 +131,93 @@ def tile_list_mlat_dl_scale_kernel(tc, x, w8_words, w8_scales, tab_words, tab_sc
                 )
             return bank
 
+        def empty(engine, result, bank, scale=None):
+            if engine == "scalar" and scale:
+                nc.scalar.activation(out=result, in_=bank, func=COPY, scale=scale)
+            elif engine == "scalar":
+                nc.scalar.copy(out=result, in_=bank)
+            elif scale:
+                nc.vector.tensor_scalar(out=result, in0=bank, scalar1=scale, scalar2=None, op0=MULT)
+            else:
+                nc.vector.tensor_copy(out=result, in_=bank)
+
         def leave_bank(mt, bank, engine, after=None):
             grouped = tile("qa_grouped%d" % mt, [P, P, PACK], BF16, after)
-            if engine == "scalar":
-                nc.scalar.copy(out=grouped[:], in_=bank[:].rearrange("p i m -> p m i"))
-            else:
-                nc.vector.tensor_copy(out=grouped[:], in_=bank[:].rearrange("p i m -> p m i"))
+            empty(engine, grouped[:], bank[:].rearrange("p i m -> p m i"))
             return grouped
 
-        qa_bank = [project(mt) for mt in range(TILES)]
-        qa_grouped = [leave_bank(mt, qa_bank[mt], "scalar") for mt in range(TILES - 1)]
-
-        under_second_half = BANK // P
-        qa_plane = [lower_plane(v_plane, under_second_half + t) for t in range(TILES - 1)]
+        qa_bank = [project(mt) for mt in range(EARLY)]
+        qa_grouped = [leave_bank(mt, qa_bank[mt], "scalar") for mt in range(EARLY)]
+        qa_plane = [lower_plane(v_plane, BANK // P + t) for t in range(EARLY)]
         qa3_plane = tile("qa3_plane", [P, P], U8)
         qa_plane.append(qa3_plane[:])
-        v_codes = {}
 
-        def pieces(cols):
-            found = []
-            for h0, h1 in sorted(v_codes):
-                c0, c1 = max(h0, cols.start), min(h1, cols.stop)
-                if c0 < c1:
-                    found.append(((c0, c1), v_codes[(h0, h1)][:, c0 - h0 : c1 - h0]))
-            return found
+        def scores(mt, h, result, engine):
+            bank = next_bank([P, BANK])
+            nc.tensor.matmul_mx(
+                out=bank[:], lhsT=qa_codes[mt][:].bitcast(FP8X4), lhsT_scale=qa_plane[mt],
+                rhs=v_codes[h][:].bitcast(FP8X4), rhs_scale=v_plane[:, half(h)], start=True, stop=True,
+            )
+            empty(engine, result, bank[:], SCORE_SCALE)
 
-        def scores(mt, cols, result, engine):
-            bank = next_bank([P, cols.stop - cols.start])
-            for (c0, c1), codes in pieces(cols):
-                nc.tensor.matmul_mx(
-                    out=bank[:, c0 - cols.start : c1 - cols.start], lhsT=qa_codes[mt][:].bitcast(FP8X4), lhsT_scale=qa_plane[mt],
-                    rhs=codes.bitcast(FP8X4), rhs_scale=v_plane[:, c0:c1], start=True, stop=True,
-                )
-            if engine == "scalar":
-                nc.scalar.activation(out=result, in_=bank[:], func=COPY, scale=SCORE_SCALE)
-            else:
-                nc.vector.tensor_scalar(out=result, in0=bank[:], scalar1=SCORE_SCALE, scalar2=None, op0=MULT)
+        def scores_half(mt, h, engine="scalar", after=None):
+            result = tile("scores%d_%d" % (mt, h), [P, BANK], F32, after)
+            scores(mt, h, result[:], engine)
+            nc.sync.dma_start(out=out_0[mt * P : (mt + 1) * P, half(h)], in_=result[:])
 
-        def scores_part(mt, cols, parts=1):
-            result = tile("scores%d_%d" % (mt, cols.start), [P, cols.stop - cols.start], F32)
-            width = (cols.stop - cols.start) // parts
-            for c0 in range(cols.start, cols.stop, width):
-                scores(mt, slice(c0, c0 + width), result[:, c0 - cols.start : c0 - cols.start + width], "scalar")
-            nc.sync.dma_start(out=out_0[mt * P : (mt + 1) * P, cols], in_=result[:])
-
-        def scores_whole(mt, after):
+        def scores_whole(mt, engines, after=None):
             result = tile("scores%d" % mt, [P, J], F32, after)
-            scores(mt, half(0), result[:, half(0)], "scalar")
-            scores(mt, half(1), result[:, half(1)], "vector")
+            for h in range(2):
+                scores(mt, h, result[:, half(h)], engines[h])
             nc.sync.dma_start(out=out_0[mt * P : (mt + 1) * P, :], in_=result[:])
 
-        gather_words(half(0))
-        qa_codes = [quantize("qa%d" % mt, qa_grouped[mt], qa_plane[mt]) for mt in range(TILES - 1)]
-        gather_words(half(1), after="qa_grouped0")
-        for mt in range(TILES - 1):
-            scores_part(mt, half(0))
-        qa_grouped.append(leave_bank(3, qa_bank[3], "vector", after="qa_grouped1"))
-        for mt in range(TILES - 1):
-            scores_part(mt, half(1))
-        qa_codes.append(quantize("qa3", qa_grouped[3], qa_plane[3]))
+        x_grouped.append(interleave("x_grouped3", "scalar", x_late, 0, P, after="v_rows"))
+        v_codes = [gather_words(0)]
+        qa_codes = [quantize("qa%d" % mt, qa_grouped[mt], qa_plane[mt]) for mt in range(EARLY)]
+        v_codes.append(gather_words(1, after="qa_grouped1"))
+        x_codes.append(quantize("x3", x_grouped[3], x_plane[3]))
+        for mt in range(EARLY):
+            scores_half(mt, 0)
+        scores_half(0, 1)
+        qa_bank.append(project(3))
+        scores_half(1, 1)
 
-        wvd_part = [(0, P), (P, P), (2 * P, 2 * P)]
-        wvd_plane = [tile("wvd_plane%d" % g, [P, width], U8) for g, (c0, width) in enumerate(wvd_part)]
+        wvd_plane = [tile("wvd_plane%d" % g, [P, P], U8) for g in (0, 1)]
         wvd_grouped = [interleave("wvd_grouped%d" % g, "vector", wvd_raw, g * P, P) for g in (0, 1)]
         wvd_codes = [quantize("wvd%d" % g, wvd_grouped[g], wvd_plane[g][:]) for g in (0, 1)]
-        scores_whole(3, after="wvd_grouped0")
-        wvd_grouped.append(interleave("wvd_grouped2", "vector", wvd_raw, 2 * P, 2 * P))
+        scores_half(2, 1, "vector", after="wvd_grouped0")
+        qa_grouped.append(leave_bank(3, qa_bank[3], "vector", after="wvd_grouped1"))
+        wvd_grouped.append(interleave("wvd_grouped2", "vector", wvd_raw, 2 * P, P))
 
-        def values(nt):
-            g = min(nt, 2)
-            w0 = nt * P - wvd_part[g][0]
-            wvd_cols = slice(w0, w0 + P)
+        def values(nt, engines, by_halves=False):
             result = tile("values%d" % nt, [P, J], F32)
             banks = [next_bank([P, BANK]) for h in range(2)]
             for h in range(2):
-                first = True
-                for (c0, c1), codes in pieces(half(h)):
-                    width = BANK if c1 - c0 == BANK else P
-                    for b in range(0, c1 - c0, width):
-                        nc.tensor.matmul_mx(
-                            out=banks[h][:, c0 % BANK + b : c0 % BANK + b + width],
-                            lhsT=wv4_codes[:, 2 * nt * P : 2 * (nt + 1) * P].bitcast(FP4X4),
-                            lhsT_scale=wv4_plane[:, nt * P : (nt + 1) * P],
-                            rhs=codes[:, b : b + width].bitcast(FP8X4), rhs_scale=v_plane[:, c0 + b : c0 + b + width],
-                            start=first, stop=False,
-                        )
-                        first = False
+                nc.tensor.matmul_mx(
+                    out=banks[h][:], lhsT=wv4_codes[:, 2 * nt * P : 2 * (nt + 1) * P].bitcast(FP4X4),
+                    lhsT_scale=wv4_plane[:, nt * P : (nt + 1) * P],
+                    rhs=v_codes[h][:].bitcast(FP8X4), rhs_scale=v_plane[:, half(h)], start=True, stop=False,
+                )
+                nc.tensor.matmul_mx(
+                    out=banks[h][:], lhsT=wvd_codes[nt][:].bitcast(FP8X4), lhsT_scale=wvd_plane[nt][:],
+                    rhs=v_codes[h][:].bitcast(FP8X4), rhs_scale=v_plane[:, half(h)], start=False, stop=True,
+                )
             for h in range(2):
-                for (c0, c1), codes in pieces(half(h)):
-                    nc.tensor.matmul_mx(
-                        out=banks[h][:, c0 % BANK : c0 % BANK + c1 - c0],
-                        lhsT=wvd_codes[g][:, wvd_cols].bitcast(FP8X4), lhsT_scale=wvd_plane[g][:, wvd_cols],
-                        rhs=codes.bitcast(FP8X4), rhs_scale=v_plane[:, c0:c1], start=False, stop=c1 % BANK == 0,
-                    )
-            nc.scalar.copy(out=result[:, half(0)], in_=banks[0][:])
-            nc.vector.tensor_copy(out=result[:, half(1)], in_=banks[1][:])
-            nc.sync.dma_start(out=out_1[nt * P : (nt + 1) * P, :], in_=result[:])
+                empty(engines[h], result[:, half(h)], banks[h][:])
+                if by_halves:
+                    nc.sync.dma_start(out=out_1[nt * P : (nt + 1) * P, half(h)], in_=result[:, half(h)])
+            if not by_halves:
+                nc.sync.dma_start(out=out_1[nt * P : (nt + 1) * P, :], in_=result[:])
 
-        values(0)
-        wvd_codes.append(quantize("wvd2", wvd_grouped[2], wvd_plane[2][:], after="wvd0_codes"))
-        for nt in range(1, TILES):
-            values(nt)
+        both = ("scalar", "vector")
+        values(0, ("scalar", "scalar"), True)
+        qa_codes.append(quantize("qa3", qa_grouped[3], qa_plane[3], after="wvd0_codes"))
+        wvd_plane.append(tile("wvd_plane2", [P, P], U8, after="wvd_plane0"))
+        wvd_codes.append(quantize("wvd2", wvd_grouped[2], wvd_plane[2][:]))
+        wvd_grouped.append(interleave("wvd_grouped3", "vector", wvd_raw, 3 * P, P, after="wvd_grouped1"))
+        values(1, both, True)
+        wvd_plane.append(tile("wvd_plane3", [P, P], U8, after="wvd_plane1"))
+        wvd_codes.append(quantize("wvd3", wvd_grouped[3], wvd_plane[3][:]))
+        scores_whole(3, both)
+        values(2, both)
+        values(3, both)

@@ -180,12 +180,14 @@ def tile_list_mlat_dl_scale_kernel(tc, x, w8_words, w8_scales, tab_words, tab_sc
             scores_half(mt, 0)
         scores_half(0, 1)
         qa_bank.append(project(3))
-        scores_half(1, 1)
 
         wvd_plane = [tile("wvd_plane%d" % g, [P, P], U8) for g in (0, 1)]
         wvd_grouped = [interleave("wvd_grouped%d" % g, "vector", wvd_raw, g * P, P) for g in (0, 1)]
         wvd_codes = [quantize("wvd%d" % g, wvd_grouped[g], wvd_plane[g][:]) for g in (0, 1)]
-        scores_half(2, 1, "vector", after="wvd_grouped0")
+        pair = tile("scores_pair", [P, 2, BANK], F32, after="wvd_grouped0")
+        scores(1, 1, pair[:, 0, :], "scalar")
+        scores(2, 1, pair[:, 1, :], "vector")
+        nc.sync.dma_start(out=out_0[P : 3 * P, half(1)].rearrange("(t p) j -> p t j", p=P), in_=pair[:])
         qa_grouped.append(leave_bank(3, qa_bank[3], "vector", after="wvd_grouped1"))
         wvd_grouped.append(interleave("wvd_grouped2", "vector", wvd_raw, 2 * P, P))
 
@@ -210,12 +212,12 @@ def tile_list_mlat_dl_scale_kernel(tc, x, w8_words, w8_scales, tab_words, tab_sc
                 nc.sync.dma_start(out=out_1[nt * P : (nt + 1) * P, :], in_=result[:])
 
         both = ("scalar", "vector")
-        values(0, ("scalar", "scalar"), True)
+        values(0, ("scalar", "scalar"))
         qa_codes.append(quantize("qa3", qa_grouped[3], qa_plane[3], after="wvd0_codes"))
         wvd_plane.append(tile("wvd_plane2", [P, P], U8, after="wvd_plane0"))
         wvd_codes.append(quantize("wvd2", wvd_grouped[2], wvd_plane[2][:]))
         wvd_grouped.append(interleave("wvd_grouped3", "vector", wvd_raw, 3 * P, P, after="wvd_grouped1"))
-        values(1, both, True)
+        values(1, both)
         wvd_plane.append(tile("wvd_plane3", [P, P], U8, after="wvd_plane1"))
         wvd_codes.append(quantize("wvd3", wvd_grouped[3], wvd_plane[3][:]))
         scores_whole(3, both)

@@ -65,19 +65,19 @@ def tile_list_mlat_dl_scale_kernel(tc, x, w8_words, w8_scales, tab_words, tab_sc
         nc.sync.dma_start(offsets[:], offs)
         w8_raw = tile("w8_raw", [P, R], U32)
         nc.sync.dma_start(out=w8_raw[:].bitcast(I32), in_=w8_words[0].rearrange("p r i -> p (r i)").bitcast(I32))
-        load_scale_rows(w8_plane, w8_scales, W8_FIRST, (nc.sync, nc.sync, nc.scalar, nc.scalar))
         nc.sync.dma_start(out=tab_rows[0:P:8, :].bitcast(I32), in_=tab_scales[0].bitcast(I32))
+        load_scale_rows(w8_plane, w8_scales, W8_FIRST, (nc.sync, nc.sync, nc.scalar, nc.scalar))
         x_early = load_rows("x_early", x[:, 0 : EARLY * P])
         tab_codes = tile("tab_codes", [P, T], U32)
         nc.sync.dma_start(out=tab_codes[:].bitcast(I32), in_=tab_words[0].rearrange("p t i -> p (t i)").bitcast(I32))
         x_late = load_rows("x_late", x[:, EARLY * P : M])
+        v_rows = tile("v_rows", [P, J], U8)
+        nc.vector.tensor_copy(v_rows[:], tab_rows[:].indirect(offsets[:]))
         w8_sorted = tile("w8_sorted", [P, R], U8)
         nc.vector.tensor_copy(
             out=w8_sorted[:].rearrange("p (i c e) -> p c i e", i=PACK, e=16),
             in_=w8_plane[:].rearrange("p (c e i) -> p c i e", i=PACK, e=16),
         )
-        v_rows = tile("v_rows", [P, J], U8)
-        nc.vector.tensor_copy(v_rows[:], tab_rows[:].indirect(offsets[:]))
         for r in range(4):
             nc.sync.dma_start(out=v_plane[r:P:QUADRANT, :].bitcast(I32), in_=v_rows[8 * r : P : QUADRANT, :].bitcast(I32))
         wvd_raw = load_rows("wvd_raw", wvd)
@@ -117,7 +117,8 @@ def tile_list_mlat_dl_scale_kernel(tc, x, w8_words, w8_scales, tab_words, tab_sc
             in_=w8_raw[:].rearrange("p (c e i) -> p c i e", i=PACK, e=4),
         )
 
-        x_plane = [w8_plane[:, mt * P : (mt + 1) * P] for mt in range(TILES)]
+        x_planes = tile("x_planes", [P, M], U8)
+        x_plane = [x_planes[:, mt * P : (mt + 1) * P] for mt in range(TILES)]
         x_grouped = [interleave("x_grouped%d" % mt, "scalar", x_early, mt * P, P) for mt in range(EARLY)]
         x_codes = [quantize("x%d" % mt, x_grouped[mt], x_plane[mt]) for mt in range(EARLY)]
 

@@ -61,12 +61,12 @@ def tile_list_mlat_dl_scale_kernel(tc, x, w8_words, w8_scales, tab_words, tab_sc
         for cleared in (tab_rows, wv4_plane, v_plane):
             nc.vector.memset(cleared[:].bitcast(I32), 0)
 
-        offsets = keep.tile([P, J // 16], U16, name="offsets")
-        nc.sync.dma_start(offsets[:], offs)
         w8_raw = tile("w8_raw", [P, R], U32)
         nc.sync.dma_start(out=w8_raw[:].bitcast(I32), in_=w8_words[0].rearrange("p r i -> p (r i)").bitcast(I32))
+        offsets = keep.tile([P, J // 16], U16, name="offsets")
+        nc.sync.dma_start(offsets[:], offs)
         nc.sync.dma_start(out=tab_rows[0:P:8, :].bitcast(I32), in_=tab_scales[0].bitcast(I32))
-        load_scale_rows(w8_plane, w8_scales, W8_FIRST, (nc.sync, nc.sync, nc.scalar, nc.scalar))
+        load_scale_rows(w8_plane, w8_scales, W8_FIRST, (nc.scalar,) * 4)
         x_early = load_rows("x_early", x[:, 0 : EARLY * P])
         tab_codes = tile("tab_codes", [P, T], U32)
         nc.sync.dma_start(out=tab_codes[:].bitcast(I32), in_=tab_words[0].rearrange("p t i -> p (t i)").bitcast(I32))
@@ -149,9 +149,8 @@ def tile_list_mlat_dl_scale_kernel(tc, x, w8_words, w8_scales, tab_words, tab_sc
 
         qa_bank = [project(mt) for mt in range(EARLY)]
         qa_grouped = [leave_bank(mt, qa_bank[mt], "scalar") for mt in range(EARLY)]
-        qa_plane = [lower_plane(v_plane, BANK // P + t) for t in range(EARLY)]
-        qa3_plane = tile("qa3_plane", [P, P], U8)
-        qa_plane.append(qa3_plane[:])
+        qa_plane = [lower_plane(v_plane, BANK // P + t) for t in (0, 1)]
+        qa_plane.extend(tile("qa_plane%d" % mt, [P, P], U8)[:] for mt in (2, 3))
 
         def scores(mt, h, result, engine):
             bank = next_bank([P, BANK])
@@ -174,21 +173,19 @@ def tile_list_mlat_dl_scale_kernel(tc, x, w8_words, w8_scales, tab_words, tab_sc
 
         x_grouped.append(interleave("x_grouped3", "scalar", x_late, 0, P, after="v_rows"))
         v_codes = [gather_words(0)]
-        qa_codes = [quantize("qa%d" % mt, qa_grouped[mt], qa_plane[mt]) for mt in range(EARLY)]
-        v_codes.append(gather_words(1, after="qa_grouped1"))
-        x_codes.append(quantize("x3", x_grouped[3], x_plane[3]))
-        for mt in range(EARLY):
-            scores_half(mt, 0)
-        scores_half(0, 1)
+        qa_codes = [quantize("qa%d" % mt, qa_grouped[mt], qa_plane[mt]) for mt in (0, 1)]
+        v_codes.append(gather_words(1, after="qa_grouped0"))
+        qa_codes.append(quantize("qa2", qa_grouped[2], qa_plane[2], after="qa_grouped1"))
+        x_codes.append(quantize("x3", x_grouped[3], x_plane[3], after="qa_grouped2"))
+        for h in range(2):
+            for mt in (0, 1):
+                scores_half(mt, h)
         qa_bank.append(project(3))
 
         wvd_plane = [tile("wvd_plane%d" % g, [P, P], U8) for g in (0, 1)]
         wvd_grouped = [interleave("wvd_grouped%d" % g, "vector", wvd_raw, g * P, P) for g in (0, 1)]
         wvd_codes = [quantize("wvd%d" % g, wvd_grouped[g], wvd_plane[g][:]) for g in (0, 1)]
-        pair = tile("scores_pair", [P, 2, BANK], F32, after="wvd_grouped0")
-        scores(1, 1, pair[:, 0, :], "scalar")
-        scores(2, 1, pair[:, 1, :], "vector")
-        nc.sync.dma_start(out=out_0[P : 3 * P, half(1)].rearrange("(t p) j -> p t j", p=P), in_=pair[:])
+        scores_whole(2, ("scalar", "vector"), after="wvd_grouped0")
         qa_grouped.append(leave_bank(3, qa_bank[3], "vector", after="wvd_grouped1"))
         wvd_grouped.append(interleave("wvd_grouped2", "vector", wvd_raw, 2 * P, P))
 

@@ -42,7 +42,7 @@ def tile_list_mlat_dl_scale_kernel(tc, x, w8_words, w8_scales, tab_words, tab_sc
             return psum.tile(shape, F32, name="bank%d" % banks_used[-1])
 
         def tile(name, shape, dtype, after=None):
-            return keep.tile(shape, dtype, name=name, tag=after or name, align_bytes=64)
+            return keep.tile(shape, dtype, name=name, tag=after or name, align_bytes=256)
 
         def load_scale_rows(plane, rows, first, queues):
             for r in range(4):

@@ -74,7 +74,7 @@ def tile_list_mlat_dl_scale_kernel(tc, x, w8_words, w8_scales, tab_words, tab_sc
         v_rows = tile("v_rows", [P, J], U8)
         nc.vector.tensor_copy(v_rows[:], tab_rows[:].indirect(offsets[:]))
         w8_sorted = tile("w8_sorted", [P, R], U8)
-        nc.vector.tensor_copy(
+        nc.gpsimd.tensor_copy(
             out=w8_sorted[:].rearrange("p (i c e) -> p c i e", i=PACK, e=16),
             in_=w8_plane[:].rearrange("p (c e i) -> p c i e", i=PACK, e=16),
         )

@@ -27,6 +27,7 @@ TILES = 4
 WVD_PART = 256
 SCORE_SCALE = 0.03125
 EARLY = 3
+WEIGHT_CODES, MOVING_PLANE, WEIGHT_PLANE = 64, 128, 192
 W8_FIRST = 12
 
 
@@ -44,6 +45,10 @@ def tile_list_mlat_dl_scale_kernel(tc, x, w8_words, w8_scales, tab_words, tab_sc
         def tile(name, shape, dtype, after=None):
             return keep.tile(shape, dtype, name=name, tag=after or name, align_bytes=256)
 
+        def shifted(name, columns, dtype, shift, after=None):
+            spare = shift // (4 if dtype == U32 else 1)
+            return tile(name, [P, spare + columns], dtype, after)[:, spare : spare + columns]
+
         def load_scale_rows(plane, rows, first, queues):
             for r in range(4):
                 queues[r].dma_start(out=plane[first + r : P : QUADRANT, :].bitcast(I32), in_=rows[0, r:BLOCKS:4, :].bitcast(I32))
@@ -54,9 +59,9 @@ def tile_list_mlat_dl_scale_kernel(tc, x, w8_words, w8_scales, tab_words, tab_sc
             return raw
 
         tab_rows = tile("tab_rows", [P, T], U8)
-        v_plane = tile("v_plane", [P, J], U8)
+        v_plane = shifted("v_plane", J, U8, MOVING_PLANE)
         w8_plane = tile("w8_plane", [P, R], U8)
-        wv4_plane = tile("wv4_plane", [P, N], U8)
+        wv4_plane = shifted("wv4_plane", N, U8, WEIGHT_PLANE)
         nc.gpsimd.memset(w8_plane[:].bitcast(I32), 0)
         for cleared in (tab_rows, wv4_plane, v_plane):
             nc.vector.memset(cleared[:].bitcast(I32), 0)
@@ -81,7 +86,7 @@ def tile_list_mlat_dl_scale_kernel(tc, x, w8_words, w8_scales, tab_words, tab_sc
         for r in range(4):
             nc.sync.dma_start(out=v_plane[r:P:QUADRANT, :].bitcast(I32), in_=v_rows[8 * r : P : QUADRANT, :].bitcast(I32))
         wvd_raw = load_rows("wvd_raw", wvd)
-        wv4_codes = tile("wv4_codes", [P, 2 * N], U8)
+        wv4_codes = shifted("wv4_codes", 2 * N, U8, WEIGHT_CODES)
         nc.sync.dma_start(out=wv4_codes[:].bitcast(I32), in_=wv4_words[0].bitcast(I32))
         load_scale_rows(wv4_plane, wv4_scales, 0, (nc.sync,) * 4)
 
@@ -96,7 +101,7 @@ def tile_list_mlat_dl_scale_kernel(tc, x, w8_words, w8_scales, tab_words, tab_sc
             return grouped
 
         def quantize(name, grouped, plane, after=None):
-            codes = tile(name + "_codes", [P, grouped.shape[1]], U32, after)
+            codes = shifted(name + "_codes", grouped.shape[1], U32, WEIGHT_CODES, after)
             nc.vector.quantize_mx(out=codes[:].bitcast(FP8X4), scales=plane, in_=grouped[:, :, :].rearrange("p c i -> p (c i)"))
             return codes
 
@@ -150,7 +155,7 @@ def tile_list_mlat_dl_scale_kernel(tc, x, w8_words, w8_scales, tab_words, tab_sc
         qa_bank = [project(mt) for mt in range(EARLY)]
         qa_grouped = [leave_bank(mt, qa_bank[mt], "scalar") for mt in range(EARLY)]
         qa_plane = [lower_plane(v_plane, BANK // P + t) for t in (0, 1)]
-        qa_plane.extend(tile("qa_plane%d" % mt, [P, P], U8)[:] for mt in (2, 3))
+        qa_plane.extend(shifted("qa_plane%d" % mt, P, U8, WEIGHT_PLANE) for mt in (2, 3))
 
         def scores(mt, h, result, engine):
             bank = next_bank([P, BANK])
@@ -182,7 +187,7 @@ def tile_list_mlat_dl_scale_kernel(tc, x, w8_words, w8_scales, tab_words, tab_sc
                 scores_half(mt, h)
         qa_bank.append(project(3))
 
-        wvd_plane = [tile("wvd_plane%d" % g, [P, P], U8) for g in (0, 1)]
+        wvd_plane = [shifted("wvd_plane%d" % g, P, U8, WEIGHT_PLANE) for g in (0, 1)]
         wvd_grouped = [interleave("wvd_grouped%d" % g, "vector", wvd_raw, g * P, P) for g in (0, 1)]
         wvd_codes = [quantize("wvd%d" % g, wvd_grouped[g], wvd_plane[g][:]) for g in (0, 1)]
         scores_whole(2, ("scalar", "vector"), after="wvd_grouped0")
@@ -212,11 +217,11 @@ def tile_list_mlat_dl_scale_kernel(tc, x, w8_words, w8_scales, tab_words, tab_sc
         both = ("scalar", "vector")
         values(0, ("scalar", "scalar"))
         qa_codes.append(quantize("qa3", qa_grouped[3], qa_plane[3], after="wvd0_codes"))
-        wvd_plane.append(tile("wvd_plane2", [P, P], U8, after="wvd_plane0"))
+        wvd_plane.append(shifted("wvd_plane2", P, U8, WEIGHT_PLANE, after="wvd_plane0"))
         wvd_codes.append(quantize("wvd2", wvd_grouped[2], wvd_plane[2][:]))
         wvd_grouped.append(interleave("wvd_grouped3", "vector", wvd_raw, 3 * P, P, after="wvd_grouped1"))
         values(1, both)
-        wvd_plane.append(tile("wvd_plane3", [P, P], U8, after="wvd_plane1"))
+        wvd_plane.append(shifted("wvd_plane3", P, U8, WEIGHT_PLANE, after="wvd_plane1"))
         wvd_codes.append(quantize("wvd3", wvd_grouped[3], wvd_plane[3][:]))
         scores_whole(3, both)
         values(2, both)

from contextlib import ExitStack

import concourse.mybir as mybir

K, R, M, T, N, J = 512, 512, 512, 2048, 512, 1024
FLOPS = 2 * K * R * M + 2 * R * M * J + 2 * 2 * R * N * J

F32 = mybir.dt.float32
BF16 = mybir.dt.bfloat16
I32 = mybir.dt.int32
U32 = mybir.dt.uint32
U16 = mybir.dt.uint16
U8 = mybir.dt.uint8
FP8X4 = mybir.dt.float8_e4m3fn_x4
FP4X4 = mybir.dt.float4_e2m1fn_x4
COPY = mybir.ActivationFunctionType.Copy
MULT = mybir.AluOpType.mult

P = 128
PACK = 4
BLOCKS = 16
QUADRANT = 32
LOWER = 4
BANK = 512
BANKS = 8
TILES = 4
WVD_PART = 256
SCORE_SCALE = 0.03125
EARLY = 3
WEIGHT_CODES, MOVING_PLANE, WEIGHT_PLANE = 64, 128, 192
W8_FIRST = 12


def tile_list_mlat_dl_scale_kernel(tc, x, w8_words, w8_scales, tab_words, tab_scales, wv4_words, wv4_scales, wvd, offs, out_0, out_1):
    nc = tc.nc
    with ExitStack() as ctx:
        keep = ctx.enter_context(tc.tile_pool(name="keep", bufs=1))
        psum = ctx.enter_context(tc.psum_pool(name="psum", bufs=1))
        banks_used = []

        def next_bank(shape):
            banks_used.append(len(banks_used) % BANKS)
            return psum.tile(shape, F32, name="bank%d" % banks_used[-1])

        def tile(name, shape, dtype, after=None):
            return keep.tile(shape, dtype, name=name, tag=after or name, align_bytes=256)

        def shifted(name, columns, dtype, shift, after=None):
            spare = shift // (4 if dtype == U32 else 1)
            return tile(name, [P, spare + columns], dtype, after)[:, spare : spare + columns]

        def load_scale_rows(plane, rows, first, queues):
            for r in range(4):
                queues[r].dma_start(out=plane[first + r : P : QUADRANT, :].bitcast(I32), in_=rows[0, r:BLOCKS:4, :].bitcast(I32))

        def load_rows(name, src):
            raw = tile(name, [P, PACK, src.shape[1]], F32)
            nc.sync.dma_start(out=raw[:], in_=src.rearrange("(p i) c -> p i c", i=PACK))
            return raw

        tab_rows = tile("tab_rows", [P, T], U8)
        v_plane = shifted("v_plane", J, U8, MOVING_PLANE)
        w8_plane = tile("w8_plane", [P, R], U8)
        wv4_plane = shifted("wv4_plane", N, U8, WEIGHT_PLANE)
        nc.gpsimd.memset(w8_plane[:].bitcast(I32), 0)
        for cleared in (tab_rows, wv4_plane, v_plane):
            nc.vector.memset(cleared[:].bitcast(I32), 0)

        w8_raw = tile("w8_raw", [P, R], U32)
        nc.sync.dma_start(out=w8_raw[:].bitcast(I32), in_=w8_words[0].rearrange("p r i -> p (r i)").bitcast(I32))
        offsets = keep.tile([P, J // 16], U16, name="offsets")
        nc.sync.dma_start(offsets[:], offs)
        nc.sync.dma_start(out=tab_rows[0:P:8, :].bitcast(I32), in_=tab_scales[0].bitcast(I32))
        load_scale_rows(w8_plane, w8_scales, W8_FIRST, (nc.scalar,) * 4)
        x_early = load_rows("x_early", x[:, 0 : EARLY * P])
        tab_codes = tile("tab_codes", [P, T], U32)
        nc.sync.dma_start(out=tab_codes[:].bitcast(I32), in_=tab_words[0].rearrange("p t i -> p (t i)").bitcast(I32))
        x_late = load_rows("x_late", x[:, EARLY * P : M])
        v_rows = tile("v_rows", [P, J], U8)
        nc.vector.tensor_copy(v_rows[:], tab_rows[:].indirect(offsets[:]))
        w8_sorted = tile("w8_sorted", [P, R], U8)
        nc.gpsimd.tensor_copy(
            out=w8_sorted[:].rearrange("p (i c e) -> p c i e", i=PACK, e=16),
            in_=w8_plane[:].rearrange("p (c e i) -> p c i e", i=PACK, e=16),
        )
        for r in range(4):
            nc.sync.dma_start(out=v_plane[r:P:QUADRANT, :].bitcast(I32), in_=v_rows[8 * r : P : QUADRANT, :].bitcast(I32))
        wvd_raw = load_rows("wvd_raw", wvd)
        wv4_codes = shifted("wv4_codes", 2 * N, U8, WEIGHT_CODES)
        nc.sync.dma_start(out=wv4_codes[:].bitcast(I32), in_=wv4_words[0].bitcast(I32))
        load_scale_rows(wv4_plane, wv4_scales, 0, (nc.sync,) * 4)

        def interleave(name, engine, raw, c0, width, after=None):
            grouped = tile(name, [P, width, PACK], BF16, after)
            dst = grouped[:].rearrange("p (c e) i -> p c i e", e=4)
            src = raw[:, :, c0 : c0 + width].rearrange("p i (c e) -> p c i e", e=4)
            if engine == "scalar":
                nc.scalar.copy(out=dst, in_=src)
            else:
                nc.vector.tensor_copy(out=dst, in_=src)
            return grouped

        def quantize(name, grouped, plane, after=None):
            codes = shifted(name + "_codes", grouped.shape[1], U32, WEIGHT_CODES, after)
            nc.vector.quantize_mx(out=codes[:].bitcast(FP8X4), scales=plane, in_=grouped[:, :, :].rearrange("p c i -> p (c i)"))
            return codes

        def half(h):
            return slice(h * BANK, (h + 1) * BANK)

        def gather_words(h, after=None):
            picked = tile("v_codes%d" % h, [P, BANK], U32, after)
            nc.vector.tensor_copy(picked[:], tab_codes[:].indirect(offsets[:, h * BANK // 16 : (h + 1) * BANK // 16]))
            return picked

        def lower_plane(shared, t):
            return shared[LOWER:P, t * P : (t + 1) * P]

        w8_codes = tile("w8_codes", [P, R], U32)
        nc.scalar.copy(
            out=w8_codes[:].rearrange("p (i c e) -> p c i e", i=PACK, e=4),
            in_=w8_raw[:].rearrange("p (c e i) -> p c i e", i=PACK, e=4),
        )

        x_planes = tile("x_planes", [P, M], U8)
        x_plane = [x_planes[:, mt * P : (mt + 1) * P] for mt in range(TILES)]
        x_grouped = [interleave("x_grouped%d" % mt, "scalar", x_early, mt * P, P) for mt in range(EARLY)]
        x_codes = [quantize("x%d" % mt, x_grouped[mt], x_plane[mt]) for mt in range(EARLY)]

        def project(mt):
            bank = next_bank([P, PACK, P])
            for i in range(PACK):
                cols = slice(i * P, (i + 1) * P)
                nc.tensor.matmul_mx(
                    out=bank[:, i, :], lhsT=w8_codes[:, cols].bitcast(FP8X4), lhsT_scale=w8_sorted[W8_FIRST:P, cols],
                    rhs=x_codes[mt][:].bitcast(FP8X4), rhs_scale=x_plane[mt], start=True, stop=True,
                )
            return bank

        def empty(engine, result, bank, scale=None):
            if engine == "scalar" and scale:
                nc.scalar.activation(out=result, in_=bank, func=COPY, scale=scale)
            elif engine == "scalar":
                nc.scalar.copy(out=result, in_=bank)
            elif scale:
                nc.vector.tensor_scalar(out=result, in0=bank, scalar1=scale, scalar2=None, op0=MULT)
            else:
                nc.vector.tensor_copy(out=result, in_=bank)

        def leave_bank(mt, bank, engine, after=None):
            grouped = tile("qa_grouped%d" % mt, [P, P, PACK], BF16, after)
            empty(engine, grouped[:], bank[:].rearrange("p i m -> p m i"))
            return grouped

        qa_bank = [project(mt) for mt in range(EARLY)]
        qa_grouped = [leave_bank(mt, qa_bank[mt], "scalar") for mt in range(EARLY)]
        qa_plane = [lower_plane(v_plane, BANK // P + t) for t in (0, 1)]
        qa_plane.extend(shifted("qa_plane%d" % mt, P, U8, WEIGHT_PLANE) for mt in (2, 3))

        def scores(mt, h, result, engine):
            bank = next_bank([P, BANK])
            nc.tensor.matmul_mx(
                out=bank[:], lhsT=qa_codes[mt][:].bitcast(FP8X4), lhsT_scale=qa_plane[mt],
                rhs=v_codes[h][:].bitcast(FP8X4), rhs_scale=v_plane[:, half(h)], start=True, stop=True,
            )
            empty(engine, result, bank[:], SCORE_SCALE)

        def scores_half(mt, h, engine="scalar", after=None):
            result = tile("scores%d_%d" % (mt, h), [P, BANK], F32, after)
            scores(mt, h, result[:], engine)
            nc.sync.dma_start(out=out_0[mt * P : (mt + 1) * P, half(h)], in_=result[:])

        def scores_whole(mt, engines, after=None):
            result = tile("scores%d" % mt, [P, J], F32, after)
            for h in range(2):
                scores(mt, h, result[:, half(h)], engines[h])
            nc.sync.dma_start(out=out_0[mt * P : (mt + 1) * P, :], in_=result[:])

        x_grouped.append(interleave("x_grouped3", "scalar", x_late, 0, P, after="v_rows"))
        v_codes = [gather_words(0)]
        qa_codes = [quantize("qa%d" % mt, qa_grouped[mt], qa_plane[mt]) for mt in (0, 1)]
        v_codes.append(gather_words(1, after="qa_grouped0"))
        qa_codes.append(quantize("qa2", qa_grouped[2], qa_plane[2], after="qa_grouped1"))
        x_codes.append(quantize("x3", x_grouped[3], x_plane[3], after="qa_grouped2"))
        for h in range(2):
            for mt in (0, 1):
                scores_half(mt, h)
        qa_bank.append(project(3))

        wvd_plane = [shifted("wvd_plane%d" % g, P, U8, WEIGHT_PLANE) for g in (0, 1)]
        wvd_grouped = [interleave("wvd_grouped%d" % g, "vector", wvd_raw, g * P, P) for g in (0, 1)]
        wvd_codes = [quantize("wvd%d" % g, wvd_grouped[g], wvd_plane[g][:]) for g in (0, 1)]
        scores_whole(2, ("scalar", "vector"), after="wvd_grouped0")
        qa_grouped.append(leave_bank(3, qa_bank[3], "vector", after="wvd_grouped1"))
        wvd_grouped.append(interleave("wvd_grouped2", "vector", wvd_raw, 2 * P, P))

        def values(nt, engines, by_halves=False):
            result = tile("values%d" % nt, [P, J], F32)
            banks = [next_bank([P, BANK]) for h in range(2)]
            for h in range(2):
                nc.tensor.matmul_mx(
                    out=banks[h][:], lhsT=wv4_codes[:, 2 * nt * P : 2 * (nt + 1) * P].bitcast(FP4X4),
                    lhsT_scale=wv4_plane[:, nt * P : (nt + 1) * P],
                    rhs=v_codes[h][:].bitcast(FP8X4), rhs_scale=v_plane[:, half(h)], start=True, stop=False,
                )
                nc.tensor.matmul_mx(
                    out=banks[h][:], lhsT=wvd_codes[nt][:].bitcast(FP8X4), lhsT_scale=wvd_plane[nt][:],
                    rhs=v_codes[h][:].bitcast(FP8X4), rhs_scale=v_plane[:, half(h)], start=False, stop=True,
                )
            for h in range(2):
                empty(engines[h], result[:, half(h)], banks[h][:])
                if by_halves:
                    nc.sync.dma_start(out=out_1[nt * P : (nt + 1) * P, half(h)], in_=result[:, half(h)])
            if not by_halves:
                nc.sync.dma_start(out=out_1[nt * P : (nt + 1) * P, :], in_=result[:])

        both = ("scalar", "vector")
        values(0, ("scalar", "scalar"))
        qa_codes.append(quantize("qa3", qa_grouped[3], qa_plane[3], after="wvd0_codes"))
        wvd_plane.append(shifted("wvd_plane2", P, U8, WEIGHT_PLANE, after="wvd_plane0"))
        wvd_codes.append(quantize("wvd2", wvd_grouped[2], wvd_plane[2][:]))
        wvd_grouped.append(interleave("wvd_grouped3", "vector", wvd_raw, 3 * P, P, after="wvd_grouped1"))
        values(1, both)
        wvd_plane.append(shifted("wvd_plane3", P, U8, WEIGHT_PLANE, after="wvd_plane1"))
        wvd_codes.append(quantize("wvd3", wvd_grouped[3], wvd_plane[3][:]))
        scores_whole(3, both)
        values(2, both)
        values(3, both)
